import numpy as np
import ml_dtypes


def mxq(x, axis, fmt="e4m3"):
    dtype, down = {"e4m3": (ml_dtypes.float8_e4m3fn, 7), "e5m2": (ml_dtypes.float8_e5m2, 14)}[fmt]
    v = np.moveaxis(np.asarray(x, np.float32).astype(ml_dtypes.bfloat16).astype(np.float64), axis, -1)
    blocks = v.reshape(v.shape[:-1] + (-1, 32))
    amax = np.abs(blocks).max(-1, keepdims=True)
    byte = np.maximum(np.where(amax > 0, np.frexp(amax)[1] - 1 + 127, 0) - down, 1)
    scale = np.exp2(byte - 127.0)
    codes = (blocks / scale).astype(np.float32).astype(dtype).astype(np.float64)
    return np.moveaxis((codes * scale).reshape(v.shape), -1, axis)


WIDE = False


def mx_kscale(k):
    if not WIDE:
        return np.ones(k)
    levels = np.array([10, -10, 5, -5, 0])
    if k % 512:
        return np.exp2(np.random.permutation(np.resize(levels, k // 32))).repeat(32)
    a = np.empty((k // 512, 16))
    for p in range(k // 512):
        a[p, :8] = np.random.permutation(np.resize(levels, 8))
        for g in range(8):
            far = levels[np.abs(levels - a[p, g]) >= 10]
            a[p, g + 8] = far[np.random.randint(len(far))]
    return np.exp2(a.ravel()).repeat(32)


def f64(x):
    return np.asarray(x).astype(np.float64)


def striped(idx):
    return np.tile(idx.reshape(-1, 16).T, (8, 1)).astype(np.uint16)


def unstriped(offs):
    return offs[:16].T.reshape(-1).astype(np.int64)


E2M1 = np.array([0.0, 0.5, 1.0, 1.5, 2.0, 3.0, 4.0, 6.0, -0.0, -0.5, -1.0, -1.5, -2.0, -3.0, -4.0, -6.0])


def pack_weight(w, fmt):
    k, n = w.shape
    w = f64(np.asarray(w, np.float32).astype(ml_dtypes.bfloat16)).reshape(k // 32, 32, n)
    amax = np.abs(w).max(1)
    if fmt == "e4m3":
        byte = np.frexp(amax)[1] - 1 + 127 - 7
    else:
        mant, ex = np.frexp(amax / 6.0)
        byte = np.where(mant > 0.5, ex, ex - 1) + 127
    byte = np.clip(np.where(amax > 0, byte, 1), 1, 254)
    scaled = (w * np.exp2(127.0 - byte)[:, None, :]).reshape(k, n).astype(np.float32)
    by_word = np.ascontiguousarray(scaled.reshape(k // 512, 128, 4, n).transpose(0, 1, 3, 2))
    if fmt == "e4m3":
        words = by_word.astype(ml_dtypes.float8_e4m3fn).view(np.uint8)
    else:
        c = by_word.astype(ml_dtypes.float4_e2m1fn).view(np.uint8) & 0xF
        words = (c[..., 0::2] | (c[..., 1::2] << 4)).reshape(k // 512, 128, 2 * n)
    return np.ascontiguousarray(words), np.ascontiguousarray(byte.astype(np.uint8).reshape(k // 512, 16, n))


def unpack_weight(words, scales, fmt):
    g, _, n = scales.shape
    words = np.ascontiguousarray(words).reshape(g, 128, n, -1)
    if fmt == "e4m3":
        vals = words.view(ml_dtypes.float8_e4m3fn).astype(np.float64)
    else:
        nib = np.empty((g, 128, n, 4), np.uint8)
        nib[..., 0::2] = words & 0xF
        nib[..., 1::2] = words >> 4
        vals = E2M1[nib]
    vals = vals * np.repeat(np.exp2(scales.astype(np.float64) - 127.0), 8, axis=1)[..., None]
    return vals.transpose(0, 1, 3, 2).reshape(g * 512, n)


def silu(v):
    return v / (1.0 + np.exp(-np.maximum(v, -700.0)))


K, T, E, C, H, N = 512, 1024, 16, 128, 512, 128


def by_expert(wq, xq):
    return np.concatenate([wq[e].T @ xq[:, e * C:(e + 1) * C] for e in range(E)], axis=1)


def setup_inputs():
    n = np.random.standard_normal
    s = mx_kscale(K)[:, None]
    u = mx_kscale(H)
    first = np.random.permutation(np.repeat(np.arange(E), T // E))
    second = (first + 1 + np.random.permutation(np.repeat(np.arange(E - 1), -(-T // (E - 1)))[:T])) % E
    while np.bincount(second, minlength=E).max() != T // E:
        load = np.bincount(second, minlength=E); hi, lo = int(load.argmax()), int(load.argmin())
        t = np.flatnonzero((second == hi) & (first != lo))[0]; second[t] = lo
    slot_token = np.empty(E * C, np.int64); pos = np.empty((2, T), np.int64); fill = np.zeros(E, np.int64)
    place = np.stack([np.random.permutation(C) for _ in range(E)])
    for r, deal in enumerate((first, second)):
        for t in np.random.permutation(T):
            e = deal[t]; j = e * C + place[e, fill[e]]; fill[e] += 1; slot_token[j] = t; pos[r, t] = j
    g = np.random.uniform(0.2, 0.8, T)
    w1 = [pack_weight(m, "e2m1") for m in n((E, K, H)) / np.sqrt(K) / s[None] * u[None, None, :]]
    w2 = [pack_weight(m, "e2m1") for m in n((E, H, N)) / np.sqrt(H) / u[None, :, None]]
    return {
        "xT": (n((K, T)) * s).astype(np.float32),
        "w1_words": np.stack([m[0] for m in w1]),
        "w1_scales": np.stack([m[1] for m in w1]),
        "w2_words": np.stack([m[0] for m in w2]),
        "w2_scales": np.stack([m[1] for m in w2]),
        "gate": np.stack([np.tile(g, (N, 1)), np.tile(1.0 - g, (N, 1))]).astype(np.float32),
        "offs": striped(slot_token),
        "pos1": striped(pos[0]),
        "pos2": striped(pos[1]),
    }


def reference(xT, w1_words, w1_scales, w2_words, w2_scales, gate, offs, pos1, pos2):
    idx = unstriped(offs)
    w1 = np.stack([unpack_weight(w1_words[e], w1_scales[e], "e2m1") for e in range(E)])
    w2 = np.stack([unpack_weight(w2_words[e], w2_scales[e], "e2m1") for e in range(E)])
    xq = mxq(f64(xT)[:, idx], 0, "e4m3")
    h = silu(by_expert(w1, xq))
    y = by_expert(w2, mxq(h, 0, "e4m3"))
    return f64(gate[0]) * y[:, unstriped(pos1)] + f64(gate[1]) * y[:, unstriped(pos2)]

@@ -1,0 +1,253 @@
+from contextlib import ExitStack
+
+import concourse.mybir as mybir
+from concourse.masks import make_identity
+
+K, T, E, C, H, N = 512, 1024, 16, 128, 512, 128
+S = E * C
+P = 128
+FLOPS = 2 * K * H * S + 2 * H * N * S
+
+F32 = mybir.dt.float32
+BF16 = mybir.dt.bfloat16
+I32 = mybir.dt.int32
+U32 = mybir.dt.uint32
+U16 = mybir.dt.uint16
+U8 = mybir.dt.uint8
+FP8X4 = mybir.dt.float8_e4m3fn_x4
+FP4X4 = mybir.dt.float4_e2m1fn_x4
+SILU = mybir.ActivationFunctionType.Silu
+MULT = mybir.AluOpType.mult
+ADD = mybir.AluOpType.add
+
+X_CHUNKS = [256,256,256,256]
+X_VECTOR = [160,160,160,160]
+UNITS = [1,1,2,2,2,2,2,2,2]
+GROUPS = [1,1,2,2,2,2,2,2,2]
+T_ENG = "SSSSSSSSS"
+Y_ENG = "VVVVVVVVV"
+LT, LQ, LY, LEAD = 2, 3, 4, 2
+PERM = "SQYGF"
+TAIL = [512,384,128]
+
+
+def tile_moe_pln_mlp_silu_kernel(
+    tc, xT, w1_words, w1_scales, w2_words, w2_scales, gate, offs, pos1, pos2, out
+):
+    nc = tc.nc
+    with ExitStack() as ctx:
+        lists = ctx.enter_context(tc.tile_pool(name="lists", bufs=1))
+        keep = ctx.enter_context(tc.tile_pool(name="keep", bufs=1))
+        ring = ctx.enter_context(tc.tile_pool(name="ring", bufs=3))
+        psum = ctx.enter_context(tc.psum_pool(name="psum", bufs=2))
+
+        offs_sb = lists.tile([P, S // 16], U16, name="offs_sb")
+        pos1_sb = lists.tile([P, T // 16], U16, name="pos1_sb")
+        pos2_sb = lists.tile([P, T // 16], U16, name="pos2_sb")
+
+        x_words = keep.tile([P, T], U32, name="x_words", align_bytes=64)
+        x_scales = keep.tile([P, T], U8, name="x_scales", align_bytes=64)
+        w1_sb = keep.tile([P, E, 2 * H], U8, name="w1_sb", align_bytes=64)
+        w1s_sb = keep.tile([P, E, H], U8, name="w1s_sb", align_bytes=64)
+        w2_sb = keep.tile([P, E, 2 * N], U8, name="w2_sb", align_bytes=64)
+        w2s_sb = keep.tile([P, E, N], U8, name="w2s_sb", align_bytes=64)
+        gate_sb = keep.tile([P, 2, T], F32, name="gate_sb")
+        y_sb = keep.tile([P, S], F32, name="y_sb")
+        ident = keep.tile([P, P], F32, name="ident")
+        warm = keep.tile([P, 1], F32, name="warm")
+
+        nc.sync.dma_start(offs_sb[:], offs)
+        raws = []
+        t0 = 0
+        for c, w in enumerate(X_CHUNKS):
+            raw = keep.tile([P, 4, w], F32, name=f"raw{c}")
+            nc.sync.dma_start(out=raw[:], in_=xT[:, t0 : t0 + w].rearrange("(p j) w -> p j w", j=4))
+            raws.append(raw)
+            t0 += w
+
+        nc.vector.memset(warm[:], 0.0)
+        nc.scalar.activation(warm[:], warm[:], SILU)
+        nc.gpsimd.memset(x_scales[:], 0)
+        nc.vector.memset(w1s_sb[:].rearrange("p e i -> p (e i)").bitcast(I32), 0)
+        nc.vector.memset(w2s_sb[:].rearrange("p e i -> p (e i)").bitcast(I32), 0)
+        make_identity(nc, ident[:])
+
+        def load_w1s(e0, e1):
+            for q in range(4):
+                nc.sync.dma_start(
+                    out=w1s_sb[32 * q : 32 * q + 4, e0:e1, :].bitcast(I32),
+                    in_=w1_scales[e0:e1, 0, 4 * q : 4 * q + 4, :].rearrange("e r i -> r e i").bitcast(I32),
+                )
+
+        def load_w2s(e0, e1):
+            for q in range(4):
+                nc.sync.dma_start(
+                    out=w2s_sb[32 * q : 32 * q + 4, e0:e1, :].bitcast(I32),
+                    in_=w2_scales[e0:e1, 0, 4 * q : 4 * q + 4, :].rearrange("e r i -> r e i").bitcast(I32),
+                )
+
+        def load_w1(e0, e1):
+            nc.sync.dma_start(
+                out=w1_sb[:, e0:e1, :].bitcast(I32),
+                in_=w1_words[e0:e1, 0].rearrange("e p b -> p e b").bitcast(I32),
+            )
+
+        def load_w2(e0, e1):
+            nc.sync.dma_start(
+                out=w2_sb[:, e0:e1, :].bitcast(I32),
+                in_=w2_words[e0:e1, 0].rearrange("e p b -> p e b").bitcast(I32),
+            )
+
+        load_w1s(0, 4)
+        load_w1(0, 2)
+        load_w1(2, 4)
+        load_w1s(4, 16)
+        load_w1(4, 8)
+        load_w2s(0, 16)
+        load_w2(0, 4)
+        load_w1(8, 12)
+        load_w2(4, 8)
+        load_w1(12, 16)
+        load_w2(8, 16)
+        nc.sync.dma_start(pos1_sb[:], pos1)
+        nc.sync.dma_start(pos2_sb[:], pos2)
+        nc.sync.dma_start(out=gate_sb[:, 0, :], in_=gate[0])
+        nc.sync.dma_start(out=gate_sb[:, 1, :], in_=gate[1])
+
+        t0 = 0
+        for c, w in enumerate(X_CHUNKS):
+            grouped = ring.tile([P, w, 4], BF16, name="grouped", align_bytes=64)
+            src = raws[c][:].rearrange("p j w -> p w j")
+            v = X_VECTOR[c]
+            if v > 0:
+                nc.vector.tensor_copy(out=grouped[:, :v, :], in_=src[:, :v, :])
+            if v < w:
+                nc.scalar.copy(out=grouped[:, v:, :], in_=src[:, v:, :])
+            nc.vector.quantize_mx(
+                out=x_words[:, t0 : t0 + w].bitcast(FP8X4),
+                scales=x_scales[:, t0 : t0 + w],
+                in_=grouped[:].rearrange("p w j -> p (w j)"),
+            )
+            t0 += w
+
+        starts = [sum(UNITS[:u]) for u in range(len(UNITS))]
+        g_tiles, h_tiles, hg_tiles, q_tiles = {}, {}, {}, {}
+
+        def gather(e0, e1):
+            w = (e1 - e0) * C
+            lst = offs_sb[:, e0 * C // 16 : e1 * C // 16]
+            g_words = ring.tile([P, w], U32, name="g_words", bufs=3, align_bytes=64)
+            g_scales = ring.tile([P, w], U8, name="g_scales", bufs=3, align_bytes=64)
+            nc.vector.tensor_copy(out=g_words[:], in_=x_words[:].indirect(lst))
+            nc.vector.tensor_copy(out=g_scales[:], in_=x_scales[:].indirect(lst))
+            for e in range(e0, e1):
+                slots = slice((e - e0) * C, (e - e0 + 1) * C)
+                g_tiles[e] = g_words[:, slots], g_scales[:, slots]
+
+        def first(u):
+            h_tiles[u] = []
+            for i in range(UNITS[u]):
+                e = starts[u] + i
+                words, scales = g_tiles[e]
+                a_ps = psum.tile([P, H], F32, name="a_ps", bufs=4)
+                nc.tensor.matmul_mx(
+                    out=a_ps[:],
+                    lhsT=words.bitcast(FP8X4),
+                    lhsT_scale=scales,
+                    rhs=w1_sb[:, e, :].bitcast(FP4X4),
+                    rhs_scale=w1s_sb[:, e, :],
+                    start=True,
+                    stop=True,
+                )
+                h_sb = ring.tile([P, 2, P, 2], BF16, name="h_sb", bufs=8, align_bytes=64)
+                nc.scalar.activation(h_sb[:], a_ps[:].rearrange("s (p u d) -> s u p d", u=2, d=2), SILU)
+                h_tiles[u].append(h_sb)
+
+        def turn(u):
+            w = UNITS[u] * C
+            t_ps = psum.tile([P, 2, w], F32, name="t_ps", bufs=2)
+            for i in range(UNITS[u]):
+                words = h_tiles[u][i][:].rearrange("s u p d -> s (u p d)").bitcast(F32)
+                for v in range(2):
+                    nc.tensor.transpose(t_ps[:, v, i * C : (i + 1) * C], words[:, v * P : (v + 1) * P], ident[:])
+            hg = ring.tile([P, w, 4], BF16, name="hg", align_bytes=64)
+            hg_words = hg[:].rearrange("p s j -> p (s j)").bitcast(F32).rearrange("p (s v) -> p s v", v=2)
+            if T_ENG[u] == "V":
+                nc.vector.tensor_copy(out=hg_words, in_=t_ps[:].rearrange("p v s -> p s v"))
+            else:
+                nc.scalar.copy(out=hg_words, in_=t_ps[:].rearrange("p v s -> p s v"))
+            hg_tiles[u] = hg
+
+        def quantize(u):
+            w = UNITS[u] * C
+            h_words = ring.tile([P, w], U32, name="h_words", align_bytes=64)
+            h_scales = ring.tile([P, w], U8, name="h_scales", align_bytes=64)
+            nc.vector.quantize_mx(
+                out=h_words[:].bitcast(FP8X4), scales=h_scales[:], in_=hg_tiles[u][:].rearrange("p s j -> p (s j)")
+            )
+            q_tiles[u] = h_words, h_scales
+
+        def second(u):
+            w = UNITS[u] * C
+            h_words, h_scales = q_tiles[u]
+            y_ps = psum.tile([P, w], F32, name="y_ps", bufs=2)
+            for i in range(UNITS[u]):
+                e = starts[u] + i
+                cols = slice(i * C, (i + 1) * C)
+                nc.tensor.matmul_mx(
+                    out=y_ps[:, cols],
+                    lhsT=w2_sb[:, e, :].bitcast(FP4X4),
+                    lhsT_scale=w2s_sb[:, e, :],
+                    rhs=h_words[:, cols].bitcast(FP8X4),
+                    rhs_scale=h_scales[:, cols],
+                    start=True,
+                    stop=True,
+                )
+            cols = slice(starts[u] * C, starts[u] * C + w)
+            if Y_ENG[u] == "V":
+                nc.vector.tensor_copy(out=y_sb[:, cols], in_=y_ps[:])
+            else:
+                nc.scalar.copy(out=y_sb[:, cols], in_=y_ps[:])
+
+        n = len(UNITS)
+        groups = list(GROUPS)
+        have = 0
+        for s in range(n + LY):
+            for stage in PERM:
+                if stage == "G":
+                    last = min(n - 1, s + LEAD)
+                    while have < starts[last] + UNITS[last]:
+                        gather(have, have + groups[0])
+                        have += groups.pop(0)
+                if stage == "F" and s < n:
+                    first(s)
+                if stage == "S" and 0 <= s - LT < n:
+                    turn(s - LT)
+                if stage == "Q" and 0 <= s - LQ < n:
+                    quantize(s - LQ)
+                if stage == "Y" and 0 <= s - LY < n:
+                    second(s - LY)
+
+        first_half = keep.tile([P, T], F32, name="first_half")
+        nc.vector.tensor_tensor(first_half[:], y_sb[:].indirect(pos1_sb[:]), gate_sb[:, 0, :], MULT)
+        tail_starts = [sum(TAIL[:k]) for k in range(len(TAIL))]
+        second_half = {}
+
+        def fetch(k):
+            t0, w = tail_starts[k], TAIL[k]
+            half = ring.tile([P, w], F32, name=f"half_{k}", bufs=1)
+            rows = slice(t0 // 16, (t0 + w) // 16)
+            nc.vector.tensor_tensor(half[:], y_sb[:].indirect(pos2_sb[:, rows]), gate_sb[:, 1, t0 : t0 + w], MULT)
+            second_half[k] = half
+
+        def add(k):
+            t0, w = tail_starts[k], TAIL[k]
+            o = ring.tile([P, w], F32, name=f"o_{k}", bufs=1)
+            nc.vector.tensor_tensor(o[:], first_half[:, t0 : t0 + w], second_half[k][:], ADD)
+            nc.sync.dma_start(out=out[:, t0 : t0 + w], in_=o[:])
+
+        fetch(0)
+        for k in range(1, len(TAIL)):
+            fetch(k)
+            add(k - 1)
+        add(len(TAIL) - 1)

@@ -56,7 +56,6 @@ def tile_moe_pln_mlp_silu_kernel(
         ident = keep.tile([P, P], F32, name="ident")
         warm = keep.tile([P, 1], F32, name="warm")
 
-        nc.sync.dma_start(offs_sb[:], offs)
         raws = []
         t0 = 0
         for c, w in enumerate(X_CHUNKS):
@@ -64,26 +63,28 @@ def tile_moe_pln_mlp_silu_kernel(
             nc.sync.dma_start(out=raw[:], in_=xT[:, t0 : t0 + w].rearrange("(p j) w -> p j w", j=4))
             raws.append(raw)
             t0 += w
+        nc.sync.dma_start(offs_sb[:], offs)
 
         nc.vector.memset(warm[:], 0.0)
         nc.scalar.activation(warm[:], warm[:], SILU)
         nc.gpsimd.memset(x_scales[:], 0)
-        nc.vector.memset(w1s_sb[:].rearrange("p e i -> p (e i)").bitcast(I32), 0)
+        nc.vector.memset(w1s_sb[:, 0:4, :].rearrange("p e i -> p (e i)").bitcast(I32), 0)
+        nc.vector.memset(w1s_sb[:, 4:E, :].rearrange("p e i -> p (e i)").bitcast(I32), 0)
         nc.vector.memset(w2s_sb[:].rearrange("p e i -> p (e i)").bitcast(I32), 0)
         make_identity(nc, ident[:])
 
         def load_w1s(e0, e1):
             for q in range(4):
                 nc.sync.dma_start(
-                    out=w1s_sb[32 * q : 32 * q + 4, e0:e1, :].bitcast(I32),
-                    in_=w1_scales[e0:e1, 0, 4 * q : 4 * q + 4, :].rearrange("e r i -> r e i").bitcast(I32),
+                    out=w1s_sb[q:P:32, e0:e1, :].bitcast(I32),
+                    in_=w1_scales[e0:e1, 0, q:16:4, :].rearrange("e r i -> r e i").bitcast(I32),
                 )
 
         def load_w2s(e0, e1):
             for q in range(4):
                 nc.sync.dma_start(
-                    out=w2s_sb[32 * q : 32 * q + 4, e0:e1, :].bitcast(I32),
-                    in_=w2_scales[e0:e1, 0, 4 * q : 4 * q + 4, :].rearrange("e r i -> r e i").bitcast(I32),
+                    out=w2s_sb[q:P:32, e0:e1, :].bitcast(I32),
+                    in_=w2_scales[e0:e1, 0, q:16:4, :].rearrange("e r i -> r e i").bitcast(I32),
                 )
 
         def load_w1(e0, e1):
@@ -98,19 +99,17 @@ def tile_moe_pln_mlp_silu_kernel(
                 in_=w2_words[e0:e1, 0].rearrange("e p b -> p e b").bitcast(I32),
             )
 
-        load_w1s(0, 4)
         load_w1(0, 2)
-        load_w1(2, 4)
-        load_w1s(4, 16)
-        load_w1(4, 8)
-        load_w2s(0, 16)
-        load_w2(0, 4)
-        load_w1(8, 12)
-        load_w2(4, 8)
-        load_w1(12, 16)
-        load_w2(8, 16)
         nc.sync.dma_start(pos1_sb[:], pos1)
         nc.sync.dma_start(pos2_sb[:], pos2)
+        load_w1s(0, 4)
+        load_w1(2, 6)
+        load_w2s(0, 16)
+        load_w2(0, 16)
+        load_w1s(4, 10)
+        load_w1(6, 10)
+        load_w1s(10, 16)
+        load_w1(10, 16)
         nc.sync.dma_start(out=gate_sb[:, 0, :], in_=gate[0])
         nc.sync.dma_start(out=gate_sb[:, 1, :], in_=gate[1])
 

@@ -20,15 +20,11 @@ SILU = mybir.ActivationFunctionType.Silu
 MULT = mybir.AluOpType.mult
 ADD = mybir.AluOpType.add
 
-X_CHUNKS = [256,256,256,256]
-X_VECTOR = [160,160,160,160]
-UNITS = [1,1,2,2,2,2,2,2,2]
-GROUPS = [1,1,2,2,2,2,2,2,2]
-T_ENG = "SSSSSSSSS"
-Y_ENG = "VVVVVVVVV"
-LT, LQ, LY, LEAD = 2, 3, 4, 2
-PERM = "SQYGF"
-TAIL = [512,384,128]
+X_CHUNKS = [256, 256, 256, 256]
+X_VECTOR = [160, 160, 160, 160]
+GROUPS = [1, 1, 1, 1, 2, 2, 2, 2, 2, 2]
+Q_GROUPS = [(0, 4), (4, 8), (8, 10), (10, 12), (12, 14), (14, 15), (15, 16)]
+TAIL = [512, 256, 128, 128]
 
 
 def tile_moe_pln_mlp_silu_kernel(
@@ -47,15 +43,14 @@ def tile_moe_pln_mlp_silu_kernel(
 
         x_words = keep.tile([P, T], U32, name="x_words", align_bytes=64)
         x_scales = keep.tile([P, T], U8, name="x_scales", align_bytes=64)
-        w1_sb = keep.tile([P, E, 2 * H], U8, name="w1_sb", align_bytes=64)
-        w1s_sb = keep.tile([P, E, H], U8, name="w1s_sb", align_bytes=64)
-        w2_sb = keep.tile([P, E, 2 * N], U8, name="w2_sb", align_bytes=64)
-        w2s_sb = keep.tile([P, E, N], U8, name="w2s_sb", align_bytes=64)
+        planes = [keep.tile([P, 4 * H], U8, name=f"plane{g}", align_bytes=64) for g in range(5)]
         gate_sb = keep.tile([P, 2, T], F32, name="gate_sb")
+        w1_tiles, w1s_tiles, w2_tiles, w2s_tiles = {}, {}, {}, {}
         y_sb = keep.tile([P, S], F32, name="y_sb")
         ident = keep.tile([P, P], F32, name="ident")
         warm = keep.tile([P, 1], F32, name="warm")
 
+        nc.sync.dma_start(offs_sb[:], offs)
         raws = []
         t0 = 0
         for c, w in enumerate(X_CHUNKS):
@@ -63,59 +58,49 @@ def tile_moe_pln_mlp_silu_kernel(
             nc.sync.dma_start(out=raw[:], in_=xT[:, t0 : t0 + w].rearrange("(p j) w -> p j w", j=4))
             raws.append(raw)
             t0 += w
-        nc.sync.dma_start(offs_sb[:], offs)
 
         nc.vector.memset(warm[:], 0.0)
         nc.scalar.activation(warm[:], warm[:], SILU)
-        nc.gpsimd.memset(x_scales[:], 0)
-        nc.vector.memset(w1s_sb[:, 0:4, :].rearrange("p e i -> p (e i)").bitcast(I32), 0)
-        nc.vector.memset(w1s_sb[:, 4:E, :].rearrange("p e i -> p (e i)").bitcast(I32), 0)
-        nc.vector.memset(w2s_sb[:].rearrange("p e i -> p (e i)").bitcast(I32), 0)
+        for plane in planes:
+            nc.vector.memset(plane[:].bitcast(I32), 0)
+        nc.vector.memset(x_scales[:].bitcast(I32), 0)
         make_identity(nc, ident[:])
 
-        def load_w1s(e0, e1):
-            for q in range(4):
+        def load_scales(views, plane, src, e0, e1):
+            width = src.shape[3]
+            rows = plane[:, : (e1 - e0) * width].rearrange("p (e i) -> p e i", i=width)
+            for r in range(4):
                 nc.sync.dma_start(
-                    out=w1s_sb[q:P:32, e0:e1, :].bitcast(I32),
-                    in_=w1_scales[e0:e1, 0, q:16:4, :].rearrange("e r i -> r e i").bitcast(I32),
+                    out=rows[r:P:32].bitcast(I32),
+                    in_=src[e0:e1, 0, r:16:4, :].rearrange("e q i -> q e i").bitcast(I32),
                 )
+            for e in range(e0, e1):
+                views[e] = rows[:, e - e0, :]
 
-        def load_w2s(e0, e1):
-            for q in range(4):
-                nc.sync.dma_start(
-                    out=w2s_sb[q:P:32, e0:e1, :].bitcast(I32),
-                    in_=w2_scales[e0:e1, 0, q:16:4, :].rearrange("e r i -> r e i").bitcast(I32),
-                )
-
-        def load_w1(e0, e1):
+        def load_words(views, src, e0, e1, layer):
+            words = keep.tile([P, e1 - e0, src.shape[3]], U8, name=f"words_{layer}_{e0}", align_bytes=64)
             nc.sync.dma_start(
-                out=w1_sb[:, e0:e1, :].bitcast(I32),
-                in_=w1_words[e0:e1, 0].rearrange("e p b -> p e b").bitcast(I32),
+                out=words[:].bitcast(I32), in_=src[e0:e1, 0].rearrange("e p b -> p e b").bitcast(I32)
             )
+            for e in range(e0, e1):
+                views[e] = words[:, e - e0, :]
 
-        def load_w2(e0, e1):
-            nc.sync.dma_start(
-                out=w2_sb[:, e0:e1, :].bitcast(I32),
-                in_=w2_words[e0:e1, 0].rearrange("e p b -> p e b").bitcast(I32),
-            )
-
-        load_w1(0, 2)
+        load_words(w1_tiles, w1_words, 0, 1, 1)
+        load_words(w1_tiles, w1_words, 1, 2, 1)
+        load_words(w1_tiles, w1_words, 2, 4, 1)
+        load_scales(w1s_tiles, planes[0], w1_scales, 0, 4)
+        for g in range(1, 4):
+            load_words(w1_tiles, w1_words, 4 * g, 4 * g + 4, 1)
+            load_scales(w1s_tiles, planes[g], w1_scales, 4 * g, 4 * g + 4)
+        load_scales(w2s_tiles, planes[4], w2_scales, 0, E)
+        load_words(w2_tiles, w2_words, 0, E, 2)
         nc.sync.dma_start(pos1_sb[:], pos1)
         nc.sync.dma_start(pos2_sb[:], pos2)
-        load_w1s(0, 4)
-        load_w1(2, 6)
-        load_w2s(0, 16)
-        load_w2(0, 16)
-        load_w1s(4, 10)
-        load_w1(6, 10)
-        load_w1s(10, 16)
-        load_w1(10, 16)
-        nc.sync.dma_start(out=gate_sb[:, 0, :], in_=gate[0])
-        nc.sync.dma_start(out=gate_sb[:, 1, :], in_=gate[1])
+        nc.sync.dma_start(out=gate_sb[:], in_=gate.rearrange("r p t -> p r t"))
 
         t0 = 0
         for c, w in enumerate(X_CHUNKS):
-            grouped = ring.tile([P, w, 4], BF16, name="grouped", align_bytes=64)
+            grouped = keep.tile([P, w, 4], BF16, name=f"grouped{c}", align_bytes=64)
             src = raws[c][:].rearrange("p j w -> p w j")
             v = X_VECTOR[c]
             if v > 0:
@@ -129,103 +114,127 @@ def tile_moe_pln_mlp_silu_kernel(
             )
             t0 += w
 
-        starts = [sum(UNITS[:u]) for u in range(len(UNITS))]
-        g_tiles, h_tiles, hg_tiles, q_tiles = {}, {}, {}, {}
+        banks = [psum.tile([P, H], F32, name=f"bank{b}", bufs=1) for b in range(8)]
+        g_tiles, h_tiles, t_tiles, hg_tiles, q_tiles = {}, {}, {}, {}, {}
 
         def gather(e0, e1):
             w = (e1 - e0) * C
             lst = offs_sb[:, e0 * C // 16 : e1 * C // 16]
-            g_words = ring.tile([P, w], U32, name="g_words", bufs=3, align_bytes=64)
-            g_scales = ring.tile([P, w], U8, name="g_scales", bufs=3, align_bytes=64)
+            g_words = keep.tile([P, w], U32, name=f"g_words{e0}", align_bytes=64)
+            g_scales = keep.tile([P, w], U8, name=f"g_scales{e0}", align_bytes=64)
             nc.vector.tensor_copy(out=g_words[:], in_=x_words[:].indirect(lst))
             nc.vector.tensor_copy(out=g_scales[:], in_=x_scales[:].indirect(lst))
             for e in range(e0, e1):
                 slots = slice((e - e0) * C, (e - e0 + 1) * C)
                 g_tiles[e] = g_words[:, slots], g_scales[:, slots]
 
-        def first(u):
-            h_tiles[u] = []
-            for i in range(UNITS[u]):
-                e = starts[u] + i
-                words, scales = g_tiles[e]
-                a_ps = psum.tile([P, H], F32, name="a_ps", bufs=4)
-                nc.tensor.matmul_mx(
-                    out=a_ps[:],
-                    lhsT=words.bitcast(FP8X4),
-                    lhsT_scale=scales,
-                    rhs=w1_sb[:, e, :].bitcast(FP4X4),
-                    rhs_scale=w1s_sb[:, e, :],
-                    start=True,
-                    stop=True,
-                )
-                h_sb = ring.tile([P, 2, P, 2], BF16, name="h_sb", bufs=8, align_bytes=64)
-                nc.scalar.activation(h_sb[:], a_ps[:].rearrange("s (p u d) -> s u p d", u=2, d=2), SILU)
-                h_tiles[u].append(h_sb)
-
-        def turn(u):
-            w = UNITS[u] * C
-            t_ps = psum.tile([P, 2, w], F32, name="t_ps", bufs=2)
-            for i in range(UNITS[u]):
-                words = h_tiles[u][i][:].rearrange("s u p d -> s (u p d)").bitcast(F32)
-                for v in range(2):
-                    nc.tensor.transpose(t_ps[:, v, i * C : (i + 1) * C], words[:, v * P : (v + 1) * P], ident[:])
-            hg = ring.tile([P, w, 4], BF16, name="hg", align_bytes=64)
-            hg_words = hg[:].rearrange("p s j -> p (s j)").bitcast(F32).rearrange("p (s v) -> p s v", v=2)
-            if T_ENG[u] == "V":
-                nc.vector.tensor_copy(out=hg_words, in_=t_ps[:].rearrange("p v s -> p s v"))
-            else:
-                nc.scalar.copy(out=hg_words, in_=t_ps[:].rearrange("p v s -> p s v"))
-            hg_tiles[u] = hg
-
-        def quantize(u):
-            w = UNITS[u] * C
-            h_words = ring.tile([P, w], U32, name="h_words", align_bytes=64)
-            h_scales = ring.tile([P, w], U8, name="h_scales", align_bytes=64)
-            nc.vector.quantize_mx(
-                out=h_words[:].bitcast(FP8X4), scales=h_scales[:], in_=hg_tiles[u][:].rearrange("p s j -> p (s j)")
+        def first(e, bank):
+            words, scales = g_tiles[e]
+            nc.tensor.matmul_mx(
+                out=banks[bank][:],
+                lhsT=words.bitcast(FP8X4),
+                lhsT_scale=scales,
+                rhs=w1_tiles[e].bitcast(FP4X4),
+                rhs_scale=w1s_tiles[e],
+                start=True,
+                stop=True,
             )
-            q_tiles[u] = h_words, h_scales
+            h_sb = keep.tile([P, 2, P, 2], BF16, name=f"h_sb{e}", align_bytes=64)
+            nc.scalar.activation(h_sb[:], banks[bank][:].rearrange("s (p u d) -> s u p d", u=2, d=2), SILU)
+            h_tiles[e] = h_sb
 
-        def second(u):
-            w = UNITS[u] * C
-            h_words, h_scales = q_tiles[u]
-            y_ps = psum.tile([P, w], F32, name="y_ps", bufs=2)
-            for i in range(UNITS[u]):
-                e = starts[u] + i
-                cols = slice(i * C, (i + 1) * C)
+        def turn(e0, e1, bank):
+            w = (e1 - e0) * C
+            t_ps = banks[bank][:, : 2 * w].rearrange("p (v s) -> p v s", v=2)
+            for e in range(e0, e1):
+                words = h_tiles[e][:].rearrange("s u p d -> s (u p d)").bitcast(F32)
+                for v in range(2):
+                    nc.tensor.transpose(t_ps[:, v, (e - e0) * C : (e - e0 + 1) * C], words[:, v * P : (v + 1) * P], ident[:])
+            t_tiles[e0] = t_ps
+
+        for e0, e1 in Q_GROUPS:
+            hg = keep.tile([P, (e1 - e0) * C * 4], BF16, name=f"hg{e0}", align_bytes=64)
+            for e in range(e0, e1):
+                hg_tiles[e] = hg, (e - e0) * C
+
+        def weave(e0, e1, eng):
+            hg, s0 = hg_tiles[e0]
+            w = (e1 - e0) * C
+            hg_words = hg[:, 4 * s0 : 4 * (s0 + w)].bitcast(F32).rearrange("p (s v) -> p s v", v=2)
+            src = t_tiles[e0].rearrange("p v s -> p s v")
+            if eng == "V":
+                nc.vector.tensor_copy(out=hg_words, in_=src)
+            else:
+                nc.scalar.copy(out=hg_words, in_=src)
+
+        def quantize(e0, e1):
+            w = (e1 - e0) * C
+            h_words = keep.tile([P, w], U32, name=f"h_words{e0}", align_bytes=64)
+            h_scales = keep.tile([P, w], U8, name=f"h_scales{e0}", align_bytes=64)
+            nc.vector.quantize_mx(out=h_words[:].bitcast(FP8X4), scales=h_scales[:], in_=hg_tiles[e0][0][:])
+            for e in range(e0, e1):
+                slots = slice((e - e0) * C, (e - e0 + 1) * C)
+                q_tiles[e] = h_words[:, slots], h_scales[:, slots]
+
+        def second(e0, e1, bank, eng):
+            for e in range(e0, e1):
+                words, scales = q_tiles[e]
                 nc.tensor.matmul_mx(
-                    out=y_ps[:, cols],
-                    lhsT=w2_sb[:, e, :].bitcast(FP4X4),
-                    lhsT_scale=w2s_sb[:, e, :],
-                    rhs=h_words[:, cols].bitcast(FP8X4),
-                    rhs_scale=h_scales[:, cols],
+                    out=banks[bank][:, (e - e0) * C : (e - e0 + 1) * C],
+                    lhsT=w2_tiles[e].bitcast(FP4X4),
+                    lhsT_scale=w2s_tiles[e],
+                    rhs=words.bitcast(FP8X4),
+                    rhs_scale=scales,
                     start=True,
                     stop=True,
                 )
-            cols = slice(starts[u] * C, starts[u] * C + w)
-            if Y_ENG[u] == "V":
-                nc.vector.tensor_copy(out=y_sb[:, cols], in_=y_ps[:])
+            src = banks[bank][:, : (e1 - e0) * C]
+            if eng == "V":
+                nc.vector.tensor_copy(out=y_sb[:, e0 * C : e1 * C], in_=src)
             else:
-                nc.scalar.copy(out=y_sb[:, cols], in_=y_ps[:])
+                nc.scalar.copy(out=y_sb[:, e0 * C : e1 * C], in_=src)
 
-        n = len(UNITS)
-        groups = list(GROUPS)
-        have = 0
-        for s in range(n + LY):
-            for stage in PERM:
-                if stage == "G":
-                    last = min(n - 1, s + LEAD)
-                    while have < starts[last] + UNITS[last]:
-                        gather(have, have + groups[0])
-                        have += groups.pop(0)
-                if stage == "F" and s < n:
-                    first(s)
-                if stage == "S" and 0 <= s - LT < n:
-                    turn(s - LT)
-                if stage == "Q" and 0 <= s - LQ < n:
-                    quantize(s - LQ)
-                if stage == "Y" and 0 <= s - LY < n:
-                    second(s - LY)
+        e0 = 0
+        for g in GROUPS:
+            gather(e0, e0 + g)
+            e0 += g
+
+        a_banks = [0, 1, 2, 0, 1, 2, 0, 3, 1, 2, 0, 3, 1, 2, 0, 3]
+        t_banks = [3, 4, 5, 4, 5]
+        for e in range(10):
+            first(e, a_banks[e])
+            if e % 2 == 1:
+                if e >= 3:
+                    weave(e - 3, e - 1, "S")
+                turn(e - 1, e + 1, t_banks[e // 2])
+            if e == 5:
+                quantize(0, 4)
+        quantize(4, 8)
+        weave(8, 10, "V")
+        first(10, a_banks[10])
+        first(11, a_banks[11])
+        turn(10, 12, 6)
+        quantize(8, 10)
+        weave(10, 12, "V")
+        first(12, a_banks[12])
+        second(0, 4, 1, "V")
+        quantize(10, 12)
+        first(13, a_banks[13])
+        turn(12, 14, 4)
+        weave(12, 14, "V")
+        first(14, a_banks[14])
+        turn(14, 15, 7)
+        first(15, a_banks[15])
+        turn(15, 16, 5)
+        weave(14, 15, "V")
+        quantize(12, 14)
+        weave(15, 16, "V")
+        quantize(14, 15)
+        quantize(15, 16)
+        second(4, 8, 2, "S")
+        second(8, 12, 0, "S")
+        second(12, 14, 3, "V")
+        second(14, 16, 6, "S")
 
         first_half = keep.tile([P, T], F32, name="first_half")
         nc.vector.tensor_tensor(first_half[:], y_sb[:].indirect(pos1_sb[:]), gate_sb[:, 0, :], MULT)

@@ -22,9 +22,9 @@ ADD = mybir.AluOpType.add
 
 X_CHUNKS = [256, 256, 256, 256]
 X_VECTOR = [160, 160, 160, 160]
-GROUPS = [1, 1, 1, 1, 2, 2, 2, 2, 2, 2]
-Q_GROUPS = [(0, 4), (4, 8), (8, 10), (10, 12), (12, 14), (14, 15), (15, 16)]
-TAIL = [512, 256, 128, 128]
+X_QUANT = [[256], [256], [256], [256]]
+GROUPS = [1, 1, 1, 1, 2, 2, 4, 4]
+Q_GROUPS = [(0, 4), (4, 8), (8, 12), (12, 14), (14, 15), (15, 16)]
 
 
 def tile_moe_pln_mlp_silu_kernel(
@@ -50,13 +50,15 @@ def tile_moe_pln_mlp_silu_kernel(
         ident = keep.tile([P, P], F32, name="ident")
         warm = keep.tile([P, 1], F32, name="warm")
 
-        nc.sync.dma_start(offs_sb[:], offs)
         raws = []
         t0 = 0
         for c, w in enumerate(X_CHUNKS):
             raw = keep.tile([P, 4, w], F32, name=f"raw{c}")
             nc.sync.dma_start(out=raw[:], in_=xT[:, t0 : t0 + w].rearrange("(p j) w -> p j w", j=4))
             raws.append(raw)
+            if c == 0:
+                nc.sync.dma_start(offs_sb[:], offs)
+                nc.sync.dma_start(pos1_sb[:], pos1)
             t0 += w
 
         nc.vector.memset(warm[:], 0.0)
@@ -87,31 +89,32 @@ def tile_moe_pln_mlp_silu_kernel(
 
         load_words(w1_tiles, w1_words, 0, 1, 1)
         load_words(w1_tiles, w1_words, 1, 2, 1)
-        load_words(w1_tiles, w1_words, 2, 4, 1)
         load_scales(w1s_tiles, planes[0], w1_scales, 0, 4)
+        load_words(w1_tiles, w1_words, 2, 4, 1)
         for g in range(1, 4):
             load_words(w1_tiles, w1_words, 4 * g, 4 * g + 4, 1)
             load_scales(w1s_tiles, planes[g], w1_scales, 4 * g, 4 * g + 4)
         load_scales(w2s_tiles, planes[4], w2_scales, 0, E)
         load_words(w2_tiles, w2_words, 0, E, 2)
-        nc.sync.dma_start(pos1_sb[:], pos1)
         nc.sync.dma_start(pos2_sb[:], pos2)
         nc.sync.dma_start(out=gate_sb[:], in_=gate.rearrange("r p t -> p r t"))
 
         t0 = 0
         for c, w in enumerate(X_CHUNKS):
             grouped = keep.tile([P, w, 4], BF16, name=f"grouped{c}", align_bytes=64)
-            src = raws[c][:].rearrange("p j w -> p w j")
-            v = X_VECTOR[c]
-            if v > 0:
-                nc.vector.tensor_copy(out=grouped[:, :v, :], in_=src[:, :v, :])
-            if v < w:
-                nc.scalar.copy(out=grouped[:, v:, :], in_=src[:, v:, :])
-            nc.vector.quantize_mx(
-                out=x_words[:, t0 : t0 + w].bitcast(FP8X4),
-                scales=x_scales[:, t0 : t0 + w],
-                in_=grouped[:].rearrange("p w j -> p (w j)"),
-            )
+            src = raws[c][:].rearrange("p j (c i) -> p c j i", i=4)
+            dst = grouped[:].rearrange("p (c i) j -> p c j i", i=4)
+            v = X_VECTOR[c] // 4
+            nc.vector.tensor_copy(out=dst[:, :v], in_=src[:, :v])
+            nc.scalar.copy(out=dst[:, v:], in_=src[:, v:])
+            q0 = 0
+            for q in X_QUANT[c]:
+                nc.vector.quantize_mx(
+                    out=x_words[:, t0 + q0 : t0 + q0 + q].bitcast(FP8X4),
+                    scales=x_scales[:, t0 + q0 : t0 + q0 + q],
+                    in_=grouped[:, q0 : q0 + q, :].rearrange("p w j -> p (w j)"),
+                )
+                q0 += q
             t0 += w
 
         banks = [psum.tile([P, H], F32, name=f"bank{b}", bufs=1) for b in range(8)]
@@ -201,61 +204,66 @@ def tile_moe_pln_mlp_silu_kernel(
 
         a_banks = [0, 1, 2, 0, 1, 2, 0, 3, 1, 2, 0, 3, 1, 2, 0, 3]
         t_banks = [3, 4, 5, 4, 5]
-        for e in range(10):
+        a_banks = [0, 1, 2, 0, 1, 2, 0, 3, 1, 2, 0, 3, 1, 2, 0, 3]
+        t_banks = [3, 4, 5, 4, 6, 4, 7]
+        for e in range(14):
             first(e, a_banks[e])
             if e % 2 == 1:
-                if e >= 3:
+                if e in (3, 5, 9, 13):
                     weave(e - 3, e - 1, "S")
                 turn(e - 1, e + 1, t_banks[e // 2])
-            if e == 5:
-                quantize(0, 4)
-        quantize(4, 8)
-        weave(8, 10, "V")
-        first(10, a_banks[10])
-        first(11, a_banks[11])
-        turn(10, 12, 6)
-        quantize(8, 10)
-        weave(10, 12, "V")
-        first(12, a_banks[12])
-        second(0, 4, 1, "V")
-        quantize(10, 12)
-        first(13, a_banks[13])
-        turn(12, 14, 4)
-        weave(12, 14, "V")
-        first(14, a_banks[14])
-        turn(14, 15, 7)
-        first(15, a_banks[15])
-        turn(15, 16, 5)
-        weave(14, 15, "V")
+                if e in (5, 9, 13):
+                    weave(e - 1, e + 1, "V")
+                    quantize(2 * (e // 2) - 4, 2 * (e // 2))
+            if e == 12:
+                second(0, 4, 1, "V")
         quantize(12, 14)
-        weave(15, 16, "V")
+        first(14, a_banks[14])
+        turn(14, 15, 5)
+        weave(14, 15, "V")
+        first(15, a_banks[15])
+        turn(15, 16, 4)
+        weave(15, 16, "S")
         quantize(14, 15)
         quantize(15, 16)
         second(4, 8, 2, "S")
-        second(8, 12, 0, "S")
-        second(12, 14, 3, "V")
-        second(14, 16, 6, "S")
+        second(8, 12, 3, "V")
+        second(12, 15, 4, "S")
+        second(15, 16, 6, "V")
 
-        first_half = keep.tile([P, T], F32, name="first_half")
-        nc.vector.tensor_tensor(first_half[:], y_sb[:].indirect(pos1_sb[:]), gate_sb[:, 0, :], MULT)
-        tail_starts = [sum(TAIL[:k]) for k in range(len(TAIL))]
-        second_half = {}
-
-        def fetch(k):
-            t0, w = tail_starts[k], TAIL[k]
-            half = ring.tile([P, w], F32, name=f"half_{k}", bufs=1)
+        def fetch(r, t0, w):
+            half = keep.tile([P, w], F32, name=f"half_{r}_{t0}")
             rows = slice(t0 // 16, (t0 + w) // 16)
-            nc.vector.tensor_tensor(half[:], y_sb[:].indirect(pos2_sb[:, rows]), gate_sb[:, 1, t0 : t0 + w], MULT)
-            second_half[k] = half
+            nc.vector.tensor_tensor(half[:], y_sb[:].indirect(pos_sb[r][:, rows]), gate_sb[:, r, t0 : t0 + w], MULT)
+            return half
 
-        def add(k):
-            t0, w = tail_starts[k], TAIL[k]
-            o = ring.tile([P, w], F32, name=f"o_{k}", bufs=1)
-            nc.vector.tensor_tensor(o[:], first_half[:, t0 : t0 + w], second_half[k][:], ADD)
-            nc.sync.dma_start(out=out[:, t0 : t0 + w], in_=o[:])
+        pos_sb = [pos1_sb, pos2_sb]
+        on_tensor = 512
+        blocks = [slice(b * P, (b + 1) * P) for b in range(on_tensor // P)]
+        first_half = fetch(0, 0, on_tensor)
+        second_half = [fetch(1, s0, 2 * P) for s0 in range(0, on_tensor, 2 * P)]
+        for b, cols in enumerate(blocks):
+            nc.tensor.matmul(banks[b][:, :P], first_half[:, cols], ident[:], start=True, stop=False, is_transpose=True)
+        for b in range(len(blocks)):
+            nc.tensor.matmul(
+                banks[b][:, :P], second_half[b // 2][:, blocks[b % 2]], ident[:], start=False, stop=True, is_transpose=True
+            )
+        turned = keep.tile([P, on_tensor], F32, name="turned")
+        for b, cols in enumerate(blocks):
+            nc.scalar.copy(out=turned[:, cols], in_=banks[b][:, :P])
+            nc.tensor.transpose(banks[4 + b // 2][:, blocks[b % 2]], turned[:, cols], ident[:])
+        for k in range(on_tensor // (2 * P)):
+            o = keep.tile([P, 2 * P], F32, name=f"o_turned{k}")
+            nc.scalar.copy(out=o[:], in_=banks[4 + k][:, : 2 * P])
+            nc.scalar.dma_start(out=out[:, 2 * P * k : 2 * P * (k + 1)], in_=o[:])
 
-        fetch(0)
-        for k in range(1, len(TAIL)):
-            fetch(k)
-            add(k - 1)
-        add(len(TAIL) - 1)
+        t0 = on_tensor
+        first_half = fetch(0, t0, T - t0)
+        pieces = [(t0, 256), (t0 + 256, 128), (t0 + 384, 128)]
+        second_half = [fetch(1, *pieces[0])]
+        for k, (s0, w) in enumerate(pieces):
+            if k + 1 < len(pieces):
+                second_half.append(fetch(1, *pieces[k + 1]))
+            o = keep.tile([P, w], F32, name=f"o_{s0}")
+            nc.vector.tensor_tensor(o[:], first_half[:, s0 - t0 : s0 - t0 + w], second_half[k][:], ADD)
+            nc.sync.dma_start(out=out[:, s0 : s0 + w], in_=o[:])

@@ -20,11 +20,13 @@ SILU = mybir.ActivationFunctionType.Silu
 MULT = mybir.AluOpType.mult
 ADD = mybir.AluOpType.add
 
-X_CHUNKS = [256, 256, 256, 256]
-X_VECTOR = [160, 160, 160, 160]
-X_QUANT = [[256], [256], [256], [256]]
-GROUPS = [1, 1, 1, 1, 2, 2, 4, 4]
-Q_GROUPS = [(0, 4), (4, 8), (8, 12), (12, 14), (14, 15), (15, 16)]
+CHUNK = 256
+CHUNK_ON_VECTOR = 160
+GATHERS = [(0, 1), (1, 2), (2, 3), (3, 4), (4, 6), (6, 8), (8, 10), (10, 12), (12, 16)]
+QUANTISE = [(0, 4), (4, 8), (8, 12), (12, 14), (14, 16)]
+EARLY_SCALES = 6
+ADDED_ON_TENSOR = 512
+ADDED_ON_VECTOR = [256, 128, 128]
 
 
 def tile_moe_pln_mlp_silu_kernel(
@@ -34,43 +36,42 @@ def tile_moe_pln_mlp_silu_kernel(
     with ExitStack() as ctx:
         lists = ctx.enter_context(tc.tile_pool(name="lists", bufs=1))
         keep = ctx.enter_context(tc.tile_pool(name="keep", bufs=1))
-        ring = ctx.enter_context(tc.tile_pool(name="ring", bufs=3))
-        psum = ctx.enter_context(tc.psum_pool(name="psum", bufs=2))
+        psum = ctx.enter_context(tc.psum_pool(name="psum", bufs=1))
 
         offs_sb = lists.tile([P, S // 16], U16, name="offs_sb")
-        pos1_sb = lists.tile([P, T // 16], U16, name="pos1_sb")
-        pos2_sb = lists.tile([P, T // 16], U16, name="pos2_sb")
+        pos_sb = [lists.tile([P, T // 16], U16, name=f"pos{r}_sb") for r in (1, 2)]
 
         x_words = keep.tile([P, T], U32, name="x_words", align_bytes=64)
         x_scales = keep.tile([P, T], U8, name="x_scales", align_bytes=64)
-        planes = [keep.tile([P, 4 * H], U8, name=f"plane{g}", align_bytes=64) for g in range(5)]
+        early_plane = keep.tile([P, EARLY_SCALES * H], U8, name="early_plane", align_bytes=64)
+        late_plane = keep.tile([P, (E - EARLY_SCALES) * H], U8, name="late_plane", align_bytes=64)
+        w2_plane = keep.tile([P, E * N], U8, name="w2_plane", align_bytes=64)
         gate_sb = keep.tile([P, 2, T], F32, name="gate_sb")
-        w1_tiles, w1s_tiles, w2_tiles, w2s_tiles = {}, {}, {}, {}
         y_sb = keep.tile([P, S], F32, name="y_sb")
         ident = keep.tile([P, P], F32, name="ident")
         warm = keep.tile([P, 1], F32, name="warm")
 
         raws = []
-        t0 = 0
-        for c, w in enumerate(X_CHUNKS):
-            raw = keep.tile([P, 4, w], F32, name=f"raw{c}")
-            nc.sync.dma_start(out=raw[:], in_=xT[:, t0 : t0 + w].rearrange("(p j) w -> p j w", j=4))
+        for c in range(T // CHUNK):
+            raw = keep.tile([P, 4, CHUNK], F32, name=f"raw{c}")
+            nc.sync.dma_start(out=raw[:], in_=xT[:, c * CHUNK : (c + 1) * CHUNK].rearrange("(p j) w -> p j w", j=4))
             raws.append(raw)
             if c == 0:
                 nc.sync.dma_start(offs_sb[:], offs)
-                nc.sync.dma_start(pos1_sb[:], pos1)
-            t0 += w
+                nc.sync.dma_start(pos_sb[0][:], pos1)
 
         nc.vector.memset(warm[:], 0.0)
         nc.scalar.activation(warm[:], warm[:], SILU)
-        for plane in planes:
-            nc.vector.memset(plane[:].bitcast(I32), 0)
+        nc.gpsimd.memset(late_plane[:].bitcast(I32), 0)
+        nc.vector.memset(early_plane[:].bitcast(I32), 0)
+        nc.vector.memset(w2_plane[:].bitcast(I32), 0)
         nc.vector.memset(x_scales[:].bitcast(I32), 0)
         make_identity(nc, ident[:])
 
+        w1_of, w1_scales_of, w2_of, w2_scales_of = {}, {}, {}, {}
+
         def load_scales(views, plane, src, e0, e1):
-            width = src.shape[3]
-            rows = plane[:, : (e1 - e0) * width].rearrange("p (e i) -> p e i", i=width)
+            rows = plane[:].rearrange("p (e i) -> p e i", e=e1 - e0)
             for r in range(4):
                 nc.sync.dma_start(
                     out=rows[r:P:32].bitcast(I32),
@@ -80,190 +81,180 @@ def tile_moe_pln_mlp_silu_kernel(
                 views[e] = rows[:, e - e0, :]
 
         def load_words(views, src, e0, e1, layer):
-            words = keep.tile([P, e1 - e0, src.shape[3]], U8, name=f"words_{layer}_{e0}", align_bytes=64)
-            nc.sync.dma_start(
-                out=words[:].bitcast(I32), in_=src[e0:e1, 0].rearrange("e p b -> p e b").bitcast(I32)
-            )
+            words = keep.tile([P, e1 - e0, src.shape[3]], U8, name=f"w{layer}_words{e0}", align_bytes=64)
+            nc.sync.dma_start(out=words[:].bitcast(I32), in_=src[e0:e1, 0].rearrange("e p b -> p e b").bitcast(I32))
             for e in range(e0, e1):
                 views[e] = words[:, e - e0, :]
 
-        load_words(w1_tiles, w1_words, 0, 1, 1)
-        load_words(w1_tiles, w1_words, 1, 2, 1)
-        load_scales(w1s_tiles, planes[0], w1_scales, 0, 4)
-        load_words(w1_tiles, w1_words, 2, 4, 1)
-        for g in range(1, 4):
-            load_words(w1_tiles, w1_words, 4 * g, 4 * g + 4, 1)
-            load_scales(w1s_tiles, planes[g], w1_scales, 4 * g, 4 * g + 4)
-        load_scales(w2s_tiles, planes[4], w2_scales, 0, E)
-        load_words(w2_tiles, w2_words, 0, E, 2)
-        nc.sync.dma_start(pos2_sb[:], pos2)
+        load_words(w1_of, w1_words, 0, 1, 1)
+        load_words(w1_of, w1_words, 1, 2, 1)
+        load_scales(w1_scales_of, early_plane, w1_scales, 0, EARLY_SCALES)
+        load_words(w1_of, w1_words, 2, EARLY_SCALES, 1)
+        load_scales(w1_scales_of, late_plane, w1_scales, EARLY_SCALES, E)
+        load_words(w1_of, w1_words, EARLY_SCALES, EARLY_SCALES + 4, 1)
+        load_words(w1_of, w1_words, EARLY_SCALES + 4, E, 1)
+        load_scales(w2_scales_of, w2_plane, w2_scales, 0, E)
+        load_words(w2_of, w2_words, 0, E, 2)
+        nc.sync.dma_start(pos_sb[1][:], pos2)
         nc.sync.dma_start(out=gate_sb[:], in_=gate.rearrange("r p t -> p r t"))
 
-        t0 = 0
-        for c, w in enumerate(X_CHUNKS):
-            grouped = keep.tile([P, w, 4], BF16, name=f"grouped{c}", align_bytes=64)
-            src = raws[c][:].rearrange("p j (c i) -> p c j i", i=4)
-            dst = grouped[:].rearrange("p (c i) j -> p c j i", i=4)
-            v = X_VECTOR[c] // 4
-            nc.vector.tensor_copy(out=dst[:, :v], in_=src[:, :v])
-            nc.scalar.copy(out=dst[:, v:], in_=src[:, v:])
-            q0 = 0
-            for q in X_QUANT[c]:
-                nc.vector.quantize_mx(
-                    out=x_words[:, t0 + q0 : t0 + q0 + q].bitcast(FP8X4),
-                    scales=x_scales[:, t0 + q0 : t0 + q0 + q],
-                    in_=grouped[:, q0 : q0 + q, :].rearrange("p w j -> p (w j)"),
-                )
-                q0 += q
-            t0 += w
+        for c, raw in enumerate(raws):
+            grouped = keep.tile([P, CHUNK, 4], BF16, name=f"grouped{c}", align_bytes=64)
+            src = raw[:].rearrange("p j (g i) -> p g j i", i=4)
+            dst = grouped[:].rearrange("p (g i) j -> p g j i", i=4)
+            cut = CHUNK_ON_VECTOR // 4
+            nc.vector.tensor_copy(out=dst[:, :cut], in_=src[:, :cut])
+            nc.scalar.copy(out=dst[:, cut:], in_=src[:, cut:])
+            tokens = slice(c * CHUNK, (c + 1) * CHUNK)
+            nc.vector.quantize_mx(
+                out=x_words[:, tokens].bitcast(FP8X4),
+                scales=x_scales[:, tokens],
+                in_=grouped[:].rearrange("p w j -> p (w j)"),
+            )
 
-        banks = [psum.tile([P, H], F32, name=f"bank{b}", bufs=1) for b in range(8)]
-        g_tiles, h_tiles, t_tiles, hg_tiles, q_tiles = {}, {}, {}, {}, {}
+        banks = [psum.tile([P, H], F32, name=f"bank{b}") for b in range(8)]
+        tokens_of, h_of, turned_of, woven_of, codes_of = {}, {}, {}, {}, {}
 
         def gather(e0, e1):
             w = (e1 - e0) * C
-            lst = offs_sb[:, e0 * C // 16 : e1 * C // 16]
+            entries = offs_sb[:, e0 * C // 16 : e1 * C // 16]
             g_words = keep.tile([P, w], U32, name=f"g_words{e0}", align_bytes=64)
             g_scales = keep.tile([P, w], U8, name=f"g_scales{e0}", align_bytes=64)
-            nc.vector.tensor_copy(out=g_words[:], in_=x_words[:].indirect(lst))
-            nc.vector.tensor_copy(out=g_scales[:], in_=x_scales[:].indirect(lst))
+            nc.vector.tensor_copy(out=g_words[:], in_=x_words[:].indirect(entries))
+            nc.vector.tensor_copy(out=g_scales[:], in_=x_scales[:].indirect(entries))
             for e in range(e0, e1):
                 slots = slice((e - e0) * C, (e - e0 + 1) * C)
-                g_tiles[e] = g_words[:, slots], g_scales[:, slots]
+                tokens_of[e] = g_words[:, slots], g_scales[:, slots]
 
-        def first(e, bank):
-            words, scales = g_tiles[e]
+        def first_layer(e, bank):
+            words, scales = tokens_of[e]
             nc.tensor.matmul_mx(
                 out=banks[bank][:],
                 lhsT=words.bitcast(FP8X4),
                 lhsT_scale=scales,
-                rhs=w1_tiles[e].bitcast(FP4X4),
-                rhs_scale=w1s_tiles[e],
+                rhs=w1_of[e].bitcast(FP4X4),
+                rhs_scale=w1_scales_of[e],
                 start=True,
                 stop=True,
             )
             h_sb = keep.tile([P, 2, P, 2], BF16, name=f"h_sb{e}", align_bytes=64)
-            nc.scalar.activation(h_sb[:], banks[bank][:].rearrange("s (p u d) -> s u p d", u=2, d=2), SILU)
-            h_tiles[e] = h_sb
+            nc.scalar.activation(h_sb[:], banks[bank][:].rearrange("s (p v d) -> s v p d", v=2, d=2), SILU)
+            h_of[e] = h_sb
 
-        def turn(e0, e1, bank):
-            w = (e1 - e0) * C
-            t_ps = banks[bank][:, : 2 * w].rearrange("p (v s) -> p v s", v=2)
-            for e in range(e0, e1):
-                words = h_tiles[e][:].rearrange("s u p d -> s (u p d)").bitcast(F32)
+        def turn(pair, bank):
+            turned = banks[bank][:].rearrange("p (v s) -> p v s", v=2)
+            for half, e in enumerate((2 * pair, 2 * pair + 1)):
+                words = h_of[e][:].rearrange("s v p d -> s (v p d)").bitcast(F32)
                 for v in range(2):
-                    nc.tensor.transpose(t_ps[:, v, (e - e0) * C : (e - e0 + 1) * C], words[:, v * P : (v + 1) * P], ident[:])
-            t_tiles[e0] = t_ps
+                    nc.tensor.transpose(turned[:, v, half * C : (half + 1) * C], words[:, v * P : (v + 1) * P], ident[:])
+            turned_of[pair] = turned
 
-        for e0, e1 in Q_GROUPS:
-            hg = keep.tile([P, (e1 - e0) * C * 4], BF16, name=f"hg{e0}", align_bytes=64)
-            for e in range(e0, e1):
-                hg_tiles[e] = hg, (e - e0) * C
+        for e0, e1 in QUANTISE:
+            woven = keep.tile([P, (e1 - e0) * C * 4], BF16, name=f"woven{e0}", align_bytes=64)
+            for e in range(e0, e1, 2):
+                woven_of[e // 2] = woven, (e - e0) * C
 
-        def weave(e0, e1, eng):
-            hg, s0 = hg_tiles[e0]
-            w = (e1 - e0) * C
-            hg_words = hg[:, 4 * s0 : 4 * (s0 + w)].bitcast(F32).rearrange("p (s v) -> p s v", v=2)
-            src = t_tiles[e0].rearrange("p v s -> p s v")
-            if eng == "V":
-                nc.vector.tensor_copy(out=hg_words, in_=src)
+        def copy_on(engine, dst, src):
+            if engine == "vector":
+                nc.vector.tensor_copy(out=dst, in_=src)
             else:
-                nc.scalar.copy(out=hg_words, in_=src)
+                nc.scalar.copy(out=dst, in_=src)
 
-        def quantize(e0, e1):
+        def weave(pair, engine):
+            woven, slot0 = woven_of[pair]
+            dst = woven[:, 4 * slot0 : 4 * (slot0 + 2 * C)].bitcast(F32).rearrange("p (s v) -> p s v", v=2)
+            copy_on(engine, dst, turned_of[pair].rearrange("p v s -> p s v"))
+
+        def quantise(group):
+            e0, e1 = QUANTISE[group]
             w = (e1 - e0) * C
             h_words = keep.tile([P, w], U32, name=f"h_words{e0}", align_bytes=64)
             h_scales = keep.tile([P, w], U8, name=f"h_scales{e0}", align_bytes=64)
-            nc.vector.quantize_mx(out=h_words[:].bitcast(FP8X4), scales=h_scales[:], in_=hg_tiles[e0][0][:])
+            nc.vector.quantize_mx(out=h_words[:].bitcast(FP8X4), scales=h_scales[:], in_=woven_of[e0 // 2][0][:])
             for e in range(e0, e1):
                 slots = slice((e - e0) * C, (e - e0 + 1) * C)
-                q_tiles[e] = h_words[:, slots], h_scales[:, slots]
+                codes_of[e] = h_words[:, slots], h_scales[:, slots]
 
-        def second(e0, e1, bank, eng):
+        def second_layer(group, bank, engine):
+            e0, e1 = QUANTISE[group]
             for e in range(e0, e1):
-                words, scales = q_tiles[e]
+                words, scales = codes_of[e]
                 nc.tensor.matmul_mx(
                     out=banks[bank][:, (e - e0) * C : (e - e0 + 1) * C],
-                    lhsT=w2_tiles[e].bitcast(FP4X4),
-                    lhsT_scale=w2s_tiles[e],
+                    lhsT=w2_of[e].bitcast(FP4X4),
+                    lhsT_scale=w2_scales_of[e],
                     rhs=words.bitcast(FP8X4),
                     rhs_scale=scales,
                     start=True,
                     stop=True,
                 )
-            src = banks[bank][:, : (e1 - e0) * C]
-            if eng == "V":
-                nc.vector.tensor_copy(out=y_sb[:, e0 * C : e1 * C], in_=src)
-            else:
-                nc.scalar.copy(out=y_sb[:, e0 * C : e1 * C], in_=src)
+            copy_on(engine, y_sb[:, e0 * C : e1 * C], banks[bank][:, : (e1 - e0) * C])
 
-        e0 = 0
-        for g in GROUPS:
-            gather(e0, e0 + g)
-            e0 += g
+        for e0, e1 in GATHERS:
+            gather(e0, e1)
 
-        a_banks = [0, 1, 2, 0, 1, 2, 0, 3, 1, 2, 0, 3, 1, 2, 0, 3]
-        t_banks = [3, 4, 5, 4, 5]
-        a_banks = [0, 1, 2, 0, 1, 2, 0, 3, 1, 2, 0, 3, 1, 2, 0, 3]
-        t_banks = [3, 4, 5, 4, 6, 4, 7]
-        for e in range(14):
-            first(e, a_banks[e])
+        first_bank = [e % 3 if e < 7 else (3, 1, 2, 5)[(e - 7) % 4] for e in range(E)]
+        turn_bank = [3, 4, 0, 4, 6, 4, 7, 0]
+        for e in range(E - 2):
+            first_layer(e, first_bank[e])
+            pair = e // 2
             if e % 2 == 1:
-                if e in (3, 5, 9, 13):
-                    weave(e - 3, e - 1, "S")
-                turn(e - 1, e + 1, t_banks[e // 2])
-                if e in (5, 9, 13):
-                    weave(e - 1, e + 1, "V")
-                    quantize(2 * (e // 2) - 4, 2 * (e // 2))
+                if pair == 1 or pair % 2 == 0 and pair > 0:
+                    weave(pair - 1, "scalar")
+                if pair != 2:
+                    turn(pair, turn_bank[pair])
+                if pair in (4, 6):
+                    weave(pair, "vector")
+                if pair % 2 == 0 and pair > 0:
+                    quantise(pair // 2 - 1)
+            if e == 6:
+                turn(2, turn_bank[2])
+                weave(2, "vector")
             if e == 12:
-                second(0, 4, 1, "V")
-        quantize(12, 14)
-        first(14, a_banks[14])
-        turn(14, 15, 5)
-        weave(14, 15, "V")
-        first(15, a_banks[15])
-        turn(15, 16, 4)
-        weave(15, 16, "S")
-        quantize(14, 15)
-        quantize(15, 16)
-        second(4, 8, 2, "S")
-        second(8, 12, 3, "V")
-        second(12, 15, 4, "S")
-        second(15, 16, 6, "V")
+                second_layer(0, first_bank[12], "vector")
+        quantise(3)
+        first_layer(14, first_bank[14])
+        first_layer(15, first_bank[15])
+        turn(7, turn_bank[7])
+        second_layer(1, first_bank[13], "scalar")
+        weave(7, "scalar")
+        quantise(4)
+        second_layer(2, first_bank[15], "scalar")
+        second_layer(3, turn_bank[7], "vector")
+        second_layer(4, turn_bank[4], "scalar")
 
         def fetch(r, t0, w):
-            half = keep.tile([P, w], F32, name=f"half_{r}_{t0}")
-            rows = slice(t0 // 16, (t0 + w) // 16)
-            nc.vector.tensor_tensor(half[:], y_sb[:].indirect(pos_sb[r][:, rows]), gate_sb[:, r, t0 : t0 + w], MULT)
-            return half
+            gated = keep.tile([P, w], F32, name=f"gated{r}_{t0}")
+            entries = pos_sb[r][:, t0 // 16 : (t0 + w) // 16]
+            nc.vector.tensor_tensor(gated[:], y_sb[:].indirect(entries), gate_sb[:, r, t0 : t0 + w], MULT)
+            return gated
 
-        pos_sb = [pos1_sb, pos2_sb]
-        on_tensor = 512
-        blocks = [slice(b * P, (b + 1) * P) for b in range(on_tensor // P)]
-        first_half = fetch(0, 0, on_tensor)
-        second_half = [fetch(1, s0, 2 * P) for s0 in range(0, on_tensor, 2 * P)]
+        blocks = [slice(b * P, (b + 1) * P) for b in range(ADDED_ON_TENSOR // P)]
+        first_choice = fetch(0, 0, ADDED_ON_TENSOR)
+        second_choice = [fetch(1, t0, 2 * P) for t0 in range(0, ADDED_ON_TENSOR, 2 * P)]
         for b, cols in enumerate(blocks):
-            nc.tensor.matmul(banks[b][:, :P], first_half[:, cols], ident[:], start=True, stop=False, is_transpose=True)
+            nc.tensor.matmul(banks[b][:, :P], first_choice[:, cols], ident[:], start=True, stop=False, is_transpose=True)
         for b in range(len(blocks)):
             nc.tensor.matmul(
-                banks[b][:, :P], second_half[b // 2][:, blocks[b % 2]], ident[:], start=False, stop=True, is_transpose=True
+                banks[b][:, :P], second_choice[b // 2][:, blocks[b % 2]], ident[:], start=False, stop=True, is_transpose=True
             )
-        turned = keep.tile([P, on_tensor], F32, name="turned")
+        sums = keep.tile([P, ADDED_ON_TENSOR], F32, name="sums")
+        back_banks = banks[len(blocks) :]
         for b, cols in enumerate(blocks):
-            nc.scalar.copy(out=turned[:, cols], in_=banks[b][:, :P])
-            nc.tensor.transpose(banks[4 + b // 2][:, blocks[b % 2]], turned[:, cols], ident[:])
-        for k in range(on_tensor // (2 * P)):
-            o = keep.tile([P, 2 * P], F32, name=f"o_turned{k}")
-            nc.scalar.copy(out=o[:], in_=banks[4 + k][:, : 2 * P])
-            nc.scalar.dma_start(out=out[:, 2 * P * k : 2 * P * (k + 1)], in_=o[:])
+            nc.scalar.copy(out=sums[:, cols], in_=banks[b][:, :P])
+            nc.tensor.transpose(back_banks[b // 2][:, blocks[b % 2]], sums[:, cols], ident[:])
+        for k in range(len(second_choice)):
+            result = keep.tile([P, 2 * P], F32, name=f"result_turned{k}")
+            nc.scalar.copy(out=result[:], in_=back_banks[k][:, : 2 * P])
+            nc.scalar.dma_start(out=out[:, 2 * P * k : 2 * P * (k + 1)], in_=result[:])
 
-        t0 = on_tensor
-        first_half = fetch(0, t0, T - t0)
-        pieces = [(t0, 256), (t0 + 256, 128), (t0 + 384, 128)]
-        second_half = [fetch(1, *pieces[0])]
-        for k, (s0, w) in enumerate(pieces):
-            if k + 1 < len(pieces):
-                second_half.append(fetch(1, *pieces[k + 1]))
-            o = keep.tile([P, w], F32, name=f"o_{s0}")
-            nc.vector.tensor_tensor(o[:], first_half[:, s0 - t0 : s0 - t0 + w], second_half[k][:], ADD)
-            nc.sync.dma_start(out=out[:, s0 : s0 + w], in_=o[:])
+        starts = [ADDED_ON_TENSOR + sum(ADDED_ON_VECTOR[:k]) for k in range(len(ADDED_ON_VECTOR))]
+        first_choice = fetch(0, ADDED_ON_TENSOR, T - ADDED_ON_TENSOR)
+        second_choice = [fetch(1, starts[0], ADDED_ON_VECTOR[0])]
+        for k, (t0, w) in enumerate(zip(starts, ADDED_ON_VECTOR)):
+            if k + 1 < len(starts):
+                second_choice.append(fetch(1, starts[k + 1], ADDED_ON_VECTOR[k + 1]))
+            result = keep.tile([P, w], F32, name=f"result{t0}")
+            cols = slice(t0 - ADDED_ON_TENSOR, t0 - ADDED_ON_TENSOR + w)
+            nc.vector.tensor_tensor(result[:], first_choice[:, cols], second_choice[k][:], ADD)
+            nc.sync.dma_start(out=out[:, t0 : t0 + w], in_=result[:])

@@ -50,6 +50,7 @@ def tile_moe_pln_mlp_silu_kernel(
         y_sb = keep.tile([P, S], F32, name="y_sb")
         ident = keep.tile([P, P], F32, name="ident")
         warm = keep.tile([P, 1], F32, name="warm")
+        banks = [psum.tile([P, H], F32, name=f"bank{b}") for b in range(8)]
 
         raws = []
         for c in range(T // CHUNK):
@@ -93,6 +94,25 @@ def tile_moe_pln_mlp_silu_kernel(
         load_scales(w1_scales_of, late_plane, w1_scales, EARLY_SCALES, E)
         load_words(w1_of, w1_words, EARLY_SCALES, EARLY_SCALES + 4, 1)
         load_words(w1_of, w1_words, EARLY_SCALES + 4, E, 1)
+        idle = keep.tile([P, 4 * P], BF16, name="idle", align_bytes=64)
+        idle_words = keep.tile([P, P], U32, name="idle_words", align_bytes=64)
+        idle_scales = keep.tile([P, P], U8, name="idle_scales", align_bytes=64)
+        nc.vector.memset(idle[:].bitcast(I32), 0)
+        nc.vector.quantize_mx(out=idle_words[:].bitcast(FP8X4), scales=idle_scales[:], in_=idle[:])
+
+        def warm_up(bank, words, scales):
+            nc.tensor.matmul_mx(
+                out=banks[bank][:],
+                lhsT=idle_words[:].bitcast(FP8X4),
+                lhsT_scale=idle_scales[:],
+                rhs=words.bitcast(FP4X4),
+                rhs_scale=scales,
+                start=True,
+                stop=True,
+            )
+
+        warm_up(7, w1_of[1], w2_plane[:, :H])
+        warm_up(7, w1_of[1], w2_plane[:, :H])
         load_scales(w2_scales_of, w2_plane, w2_scales, 0, E)
         load_words(w2_of, w2_words, 0, E, 2)
         nc.sync.dma_start(pos_sb[1][:], pos2)
@@ -112,7 +132,6 @@ def tile_moe_pln_mlp_silu_kernel(
                 in_=grouped[:].rearrange("p w j -> p (w j)"),
             )
 
-        banks = [psum.tile([P, H], F32, name=f"bank{b}") for b in range(8)]
         tokens_of, h_of, turned_of, woven_of, codes_of = {}, {}, {}, {}, {}
 
         def gather(e0, e1):
@@ -222,6 +241,8 @@ def tile_moe_pln_mlp_silu_kernel(
         second_layer(2, first_bank[15], "scalar")
         second_layer(3, turn_bank[7], "vector")
         second_layer(4, turn_bank[4], "scalar")
+        warm_up(first_bank[12], w1_of[15], w1_scales_of[15])
+        warm_up(first_bank[14], w1_of[15], w1_scales_of[15])
 
         def fetch(r, t0, w):
             gated = keep.tile([P, w], F32, name=f"gated{r}_{t0}")

@@ -123,14 +123,18 @@ def tile_moe_pln_mlp_silu_kernel(
             src = raw[:].rearrange("p j (g i) -> p g j i", i=4)
             dst = grouped[:].rearrange("p (g i) j -> p g j i", i=4)
             cut = CHUNK_ON_VECTOR // 4
-            nc.vector.tensor_copy(out=dst[:, :cut], in_=src[:, :cut])
+            halves = 2 if c == len(raws) - 1 else 1
+            step = CHUNK // halves
+            for g0, g1 in ((0, step // 4), (step // 4, cut)) if halves == 2 else ((0, cut),):
+                nc.vector.tensor_copy(out=dst[:, g0:g1], in_=src[:, g0:g1])
             nc.scalar.copy(out=dst[:, cut:], in_=src[:, cut:])
-            tokens = slice(c * CHUNK, (c + 1) * CHUNK)
-            nc.vector.quantize_mx(
-                out=x_words[:, tokens].bitcast(FP8X4),
-                scales=x_scales[:, tokens],
-                in_=grouped[:].rearrange("p w j -> p (w j)"),
-            )
+            for q0 in range(0, CHUNK, step):
+                tokens = slice(c * CHUNK + q0, c * CHUNK + q0 + step)
+                nc.vector.quantize_mx(
+                    out=x_words[:, tokens].bitcast(FP8X4),
+                    scales=x_scales[:, tokens],
+                    in_=grouped[:, q0 : q0 + step, :].rearrange("p w j -> p (w j)"),
+                )
 
         tokens_of, h_of, turned_of, woven_of, codes_of = {}, {}, {}, {}, {}
 
@@ -252,7 +256,8 @@ def tile_moe_pln_mlp_silu_kernel(
 
         blocks = [slice(b * P, (b + 1) * P) for b in range(ADDED_ON_TENSOR // P)]
         first_choice = fetch(0, 0, ADDED_ON_TENSOR)
-        second_choice = [fetch(1, t0, 2 * P) for t0 in range(0, ADDED_ON_TENSOR, 2 * P)]
+        widths = [min(2 * P, ADDED_ON_TENSOR - t0) for t0 in range(0, ADDED_ON_TENSOR, 2 * P)]
+        second_choice = [fetch(1, 2 * P * k, w) for k, w in enumerate(widths)]
         for b, cols in enumerate(blocks):
             nc.tensor.matmul(banks[b][:, :P], first_choice[:, cols], ident[:], start=True, stop=False, is_transpose=True)
         for b in range(len(blocks)):
@@ -264,10 +269,10 @@ def tile_moe_pln_mlp_silu_kernel(
         for b, cols in enumerate(blocks):
             nc.scalar.copy(out=sums[:, cols], in_=banks[b][:, :P])
             nc.tensor.transpose(back_banks[b // 2][:, blocks[b % 2]], sums[:, cols], ident[:])
-        for k in range(len(second_choice)):
-            result = keep.tile([P, 2 * P], F32, name=f"result_turned{k}")
-            nc.scalar.copy(out=result[:], in_=back_banks[k][:, : 2 * P])
-            nc.scalar.dma_start(out=out[:, 2 * P * k : 2 * P * (k + 1)], in_=result[:])
+        for k, w in enumerate(widths):
+            result = keep.tile([P, w], F32, name=f"result_turned{k}")
+            nc.scalar.copy(out=result[:], in_=back_banks[k][:, :w])
+            nc.scalar.dma_start(out=out[:, 2 * P * k : 2 * P * k + w], in_=result[:])
 
         starts = [ADDED_ON_TENSOR + sum(ADDED_ON_VECTOR[:k]) for k in range(len(ADDED_ON_VECTOR))]
         first_choice = fetch(0, ADDED_ON_TENSOR, T - ADDED_ON_TENSOR)
@@ -278,4 +283,5 @@ def tile_moe_pln_mlp_silu_kernel(
             result = keep.tile([P, w], F32, name=f"result{t0}")
             cols = slice(t0 - ADDED_ON_TENSOR, t0 - ADDED_ON_TENSOR + w)
             nc.vector.tensor_tensor(result[:], first_choice[:, cols], second_choice[k][:], ADD)
-            nc.sync.dma_start(out=out[:, t0 : t0 + w], in_=result[:])
+            queue = nc.scalar if k + 1 == len(starts) else nc.sync
+            queue.dma_start(out=out[:, t0 : t0 + w], in_=result[:])

@@ -94,25 +94,6 @@ def tile_moe_pln_mlp_silu_kernel(
         load_scales(w1_scales_of, late_plane, w1_scales, EARLY_SCALES, E)
         load_words(w1_of, w1_words, EARLY_SCALES, EARLY_SCALES + 4, 1)
         load_words(w1_of, w1_words, EARLY_SCALES + 4, E, 1)
-        idle = keep.tile([P, 4 * P], BF16, name="idle", align_bytes=64)
-        idle_words = keep.tile([P, P], U32, name="idle_words", align_bytes=64)
-        idle_scales = keep.tile([P, P], U8, name="idle_scales", align_bytes=64)
-        nc.vector.memset(idle[:].bitcast(I32), 0)
-        nc.vector.quantize_mx(out=idle_words[:].bitcast(FP8X4), scales=idle_scales[:], in_=idle[:])
-
-        def warm_up(bank, words, scales):
-            nc.tensor.matmul_mx(
-                out=banks[bank][:],
-                lhsT=idle_words[:].bitcast(FP8X4),
-                lhsT_scale=idle_scales[:],
-                rhs=words.bitcast(FP4X4),
-                rhs_scale=scales,
-                start=True,
-                stop=True,
-            )
-
-        warm_up(7, w1_of[1], w2_plane[:, :H])
-        warm_up(7, w1_of[1], w2_plane[:, :H])
         load_scales(w2_scales_of, w2_plane, w2_scales, 0, E)
         load_words(w2_of, w2_words, 0, E, 2)
         nc.sync.dma_start(pos_sb[1][:], pos2)
@@ -149,7 +130,7 @@ def tile_moe_pln_mlp_silu_kernel(
                 slots = slice((e - e0) * C, (e - e0 + 1) * C)
                 tokens_of[e] = g_words[:, slots], g_scales[:, slots]
 
-        def first_layer(e, bank):
+        def first_product(e, bank):
             words, scales = tokens_of[e]
             nc.tensor.matmul_mx(
                 out=banks[bank][:],
@@ -160,6 +141,9 @@ def tile_moe_pln_mlp_silu_kernel(
                 start=True,
                 stop=True,
             )
+
+        def first_layer(e, bank):
+            first_product(e, bank)
             h_sb = keep.tile([P, 2, P, 2], BF16, name=f"h_sb{e}", align_bytes=64)
             nc.scalar.activation(h_sb[:], banks[bank][:].rearrange("s (p v d) -> s v p d", v=2, d=2), SILU)
             h_of[e] = h_sb
@@ -245,8 +229,8 @@ def tile_moe_pln_mlp_silu_kernel(
         second_layer(2, first_bank[15], "scalar")
         second_layer(3, turn_bank[7], "vector")
         second_layer(4, turn_bank[4], "scalar")
-        warm_up(first_bank[12], w1_of[15], w1_scales_of[15])
-        warm_up(first_bank[14], w1_of[15], w1_scales_of[15])
+        first_product(E - 1, first_bank[12])
+        first_product(E - 1, first_bank[14])
 
         def fetch(r, t0, w):
             gated = keep.tile([P, w], F32, name=f"gated{r}_{t0}")

@@ -22,9 +22,9 @@ ADD = mybir.AluOpType.add
 
 CHUNK = 256
 CHUNK_ON_VECTOR = 160
-GATHERS = [(0, 1), (1, 2), (2, 3), (3, 4), (4, 6), (6, 8), (8, 10), (10, 12), (12, 16)]
+GATHERS = [(0, 1), (1, 2), (2, 3), (3, 4), (4, 5), (5, 6), (6, 7), (7, 8), (8, 10), (10, 12), (12, 14), (14, 16)]
 QUANTISE = [(0, 4), (4, 8), (8, 12), (12, 14), (14, 16)]
-EARLY_SCALES = 6
+EARLY_SCALES = 8
 ADDED_ON_TENSOR = 512
 ADDED_ON_VECTOR = [256, 128, 128]
 
@@ -200,37 +200,41 @@ def tile_moe_pln_mlp_silu_kernel(
         for e0, e1 in GATHERS:
             gather(e0, e1)
 
-        first_bank = [e % 3 if e < 7 else (3, 1, 2, 5)[(e - 7) % 4] for e in range(E)]
-        turn_bank = [3, 4, 0, 4, 6, 4, 7, 0]
-        for e in range(E - 2):
+        first_bank = [0, 1, 2, 3, 4, 5, 6, 7, 0, 1, 2, 7, 3, 4, 6, 0]
+        turn_bank = [3, 4, 5, 6, 1, 7, 4, 5]
+        for e in range(8):
             first_layer(e, first_bank[e])
-            pair = e // 2
-            if e % 2 == 1:
-                if pair == 1 or pair % 2 == 0 and pair > 0:
-                    weave(pair - 1, "scalar")
-                if pair != 2:
-                    turn(pair, turn_bank[pair])
-                if pair in (4, 6):
-                    weave(pair, "vector")
-                if pair % 2 == 0 and pair > 0:
-                    quantise(pair // 2 - 1)
-            if e == 6:
-                turn(2, turn_bank[2])
-                weave(2, "vector")
+        for pair in range(4):
+            turn(pair, turn_bank[pair])
+        weave(0, "scalar")
+        weave(1, "scalar")
+        weave(3, "scalar")
+        weave(2, "vector")
+        quantise(0)
+        for e in range(8, E):
+            first_layer(e, first_bank[e])
             if e == 12:
-                second_layer(0, first_bank[12], "vector")
-        quantise(3)
-        first_layer(14, first_bank[14])
-        first_layer(15, first_bank[15])
+                turn(4, turn_bank[4])
+                weave(4, "vector")
+                quantise(1)
+            if e == 14:
+                turn(5, turn_bank[5])
+                weave(5, "vector")
+        turn(6, turn_bank[6])
         turn(7, turn_bank[7])
-        second_layer(1, first_bank[13], "scalar")
+        weave(6, "scalar")
         weave(7, "scalar")
-        quantise(4)
-        second_layer(2, first_bank[15], "scalar")
-        second_layer(3, turn_bank[7], "vector")
-        second_layer(4, turn_bank[4], "scalar")
+        quantise(2)
         first_product(E - 1, first_bank[12])
+        second_layer(0, first_bank[12], "vector")
+        quantise(3)
+        quantise(4)
         first_product(E - 1, first_bank[14])
+        second_layer(1, first_bank[14], "scalar")
+        first_product(E - 1, first_bank[15])
+        second_layer(2, first_bank[15], "scalar")
+        second_layer(3, turn_bank[4], "scalar")
+        second_layer(4, turn_bank[5], "vector")
 
         def fetch(r, t0, w):
             gated = keep.tile([P, w], F32, name=f"gated{r}_{t0}")

@@ -24,7 +24,9 @@ CHUNK = 256
 CHUNK_ON_VECTOR = 160
 GATHERS = [(0, 1), (1, 2), (2, 3), (3, 4), (4, 5), (5, 6), (6, 7), (7, 8), (8, 10), (10, 12), (12, 14), (14, 16)]
 QUANTISE = [(0, 4), (4, 8), (8, 12), (12, 14), (14, 16)]
-EARLY_SCALES = 8
+EARLY_GATE = 32
+WARM_COLUMNS = 256
+SCALE_GROUPS = [(0, 4), (4, 8), (8, 16)]
 ADDED_ON_TENSOR = 512
 ADDED_ON_VECTOR = [256, 128, 128]
 
@@ -43,8 +45,7 @@ def tile_moe_pln_mlp_silu_kernel(
 
         x_words = keep.tile([P, T], U32, name="x_words", align_bytes=64)
         x_scales = keep.tile([P, T], U8, name="x_scales", align_bytes=64)
-        early_plane = keep.tile([P, EARLY_SCALES * H], U8, name="early_plane", align_bytes=64)
-        late_plane = keep.tile([P, (E - EARLY_SCALES) * H], U8, name="late_plane", align_bytes=64)
+        w1_planes = [keep.tile([P, (e1 - e0) * H], U8, name=f"w1_plane{e0}", align_bytes=64) for e0, e1 in SCALE_GROUPS]
         w2_plane = keep.tile([P, E * N], U8, name="w2_plane", align_bytes=64)
         gate_sb = keep.tile([P, 2, T], F32, name="gate_sb")
         y_sb = keep.tile([P, S], F32, name="y_sb")
@@ -52,6 +53,7 @@ def tile_moe_pln_mlp_silu_kernel(
         warm = keep.tile([P, 1], F32, name="warm")
         banks = [psum.tile([P, H], F32, name=f"bank{b}") for b in range(8)]
 
+        gate_rows = gate.rearrange("r p t -> p r t")
         raws = []
         for c in range(T // CHUNK):
             raw = keep.tile([P, 4, CHUNK], F32, name=f"raw{c}")
@@ -59,12 +61,13 @@ def tile_moe_pln_mlp_silu_kernel(
             raws.append(raw)
             if c == 0:
                 nc.sync.dma_start(offs_sb[:], offs)
-                nc.sync.dma_start(pos_sb[0][:], pos1)
+                nc.sync.dma_start(out=gate_sb[:, :, :EARLY_GATE], in_=gate_rows[:, :, :EARLY_GATE])
 
         nc.vector.memset(warm[:], 0.0)
         nc.scalar.activation(warm[:], warm[:], SILU)
-        nc.gpsimd.memset(late_plane[:].bitcast(I32), 0)
-        nc.vector.memset(early_plane[:].bitcast(I32), 0)
+        nc.gpsimd.memset(w1_planes[2][:].bitcast(I32), 0)
+        nc.vector.memset(w1_planes[0][:].bitcast(I32), 0)
+        nc.vector.memset(w1_planes[1][:].bitcast(I32), 0)
         nc.vector.memset(w2_plane[:].bitcast(I32), 0)
         nc.vector.memset(x_scales[:].bitcast(I32), 0)
         make_identity(nc, ident[:])
@@ -89,15 +92,36 @@ def tile_moe_pln_mlp_silu_kernel(
 
         load_words(w1_of, w1_words, 0, 1, 1)
         load_words(w1_of, w1_words, 1, 2, 1)
-        load_scales(w1_scales_of, early_plane, w1_scales, 0, EARLY_SCALES)
-        load_words(w1_of, w1_words, 2, EARLY_SCALES, 1)
-        load_scales(w1_scales_of, late_plane, w1_scales, EARLY_SCALES, E)
-        load_words(w1_of, w1_words, EARLY_SCALES, EARLY_SCALES + 4, 1)
-        load_words(w1_of, w1_words, EARLY_SCALES + 4, E, 1)
+        load_scales(w1_scales_of, w1_planes[0], w1_scales, *SCALE_GROUPS[0])
+        load_words(w1_of, w1_words, 2, 4, 1)
+        load_scales(w1_scales_of, w1_planes[1], w1_scales, *SCALE_GROUPS[1])
+        load_words(w1_of, w1_words, 4, 8, 1)
+        load_scales(w1_scales_of, w1_planes[2], w1_scales, *SCALE_GROUPS[2])
+        load_words(w1_of, w1_words, 8, 12, 1)
+        load_words(w1_of, w1_words, 12, 16, 1)
         load_scales(w2_scales_of, w2_plane, w2_scales, 0, E)
         load_words(w2_of, w2_words, 0, E, 2)
+        nc.sync.dma_start(pos_sb[0][:], pos1)
         nc.sync.dma_start(pos_sb[1][:], pos2)
-        nc.sync.dma_start(out=gate_sb[:], in_=gate.rearrange("r p t -> p r t"))
+        nc.sync.dma_start(out=gate_sb[:, :, EARLY_GATE:], in_=gate_rows[:, :, EARLY_GATE:])
+
+        spare = keep.tile([P, 4 * WARM_COLUMNS // EARLY_GATE, EARLY_GATE], BF16, name="spare", align_bytes=64)
+        spare_words = keep.tile([P, WARM_COLUMNS], U32, name="spare_words", align_bytes=64)
+        spare_scales = keep.tile([P, WARM_COLUMNS], U8, name="spare_scales", align_bytes=64)
+        nc.scalar.copy(out=spare[:], in_=gate_sb[:, 0:1, :EARLY_GATE].to_broadcast(list(spare.shape)))
+        nc.vector.quantize_mx(
+            out=spare_words[:].bitcast(FP8X4), scales=spare_scales[:], in_=spare[:].rearrange("p a b -> p (a b)")
+        )
+        for rep in range(4):
+            nc.tensor.matmul_mx(
+                out=banks[7][:, :WARM_COLUMNS],
+                lhsT=w1_of[0][:, : 2 * P].bitcast(FP4X4),
+                lhsT_scale=spare_scales[:, :P],
+                rhs=spare_words[:].bitcast(FP8X4),
+                rhs_scale=spare_scales[:],
+                start=True,
+                stop=True,
+            )
 
         for c, raw in enumerate(raws):
             grouped = keep.tile([P, CHUNK, 4], BF16, name=f"grouped{c}", align_bytes=64)
@@ -200,8 +224,8 @@ def tile_moe_pln_mlp_silu_kernel(
         for e0, e1 in GATHERS:
             gather(e0, e1)
 
-        first_bank = [0, 1, 2, 3, 4, 5, 6, 7, 0, 1, 2, 7, 3, 4, 6, 0]
-        turn_bank = [3, 4, 5, 6, 1, 7, 4, 5]
+        first_bank = [0, 1, 2, 3, 4, 5, 6, 7, 0, 1, 2, 3, 5, 6, 7, 0]
+        turn_bank = [5, 6, 4, 7, 1, 3, 6, 4]
         for e in range(8):
             first_layer(e, first_bank[e])
         for pair in range(4):

@@ -22,11 +22,13 @@ ADD = mybir.AluOpType.add
 
 CHUNK = 256
 CHUNK_ON_VECTOR = 160
-GATHERS = [(0, 1), (1, 2), (2, 3), (3, 4), (4, 5), (5, 6), (6, 7), (7, 8), (8, 10), (10, 12), (12, 14), (14, 16)]
+HALF = E // 2
+GATHERS = [(e, e + 1) for e in range(HALF)] + [(e, e + 2) for e in range(HALF, E, 2)]
 QUANTISE = [(0, 4), (4, 8), (8, 12), (12, 14), (14, 16)]
-EARLY_GATE = 32
-WARM_COLUMNS = 256
 SCALE_GROUPS = [(0, 4), (4, 8), (8, 16)]
+WARM_PASSES = 4
+WARM_COLUMNS = 256
+EARLY_GATE = 32
 ADDED_ON_TENSOR = 512
 ADDED_ON_VECTOR = [256, 128, 128]
 
@@ -50,21 +52,19 @@ def tile_moe_pln_mlp_silu_kernel(
         gate_sb = keep.tile([P, 2, T], F32, name="gate_sb")
         y_sb = keep.tile([P, S], F32, name="y_sb")
         ident = keep.tile([P, P], F32, name="ident")
-        warm = keep.tile([P, 1], F32, name="warm")
+        table_warm = keep.tile([P, 1], F32, name="table_warm")
         banks = [psum.tile([P, H], F32, name=f"bank{b}") for b in range(8)]
 
-        gate_rows = gate.rearrange("r p t -> p r t")
+        nc.sync.dma_start(out=gate_sb[:, 0, :EARLY_GATE], in_=gate[0, :, :EARLY_GATE])
         raws = []
         for c in range(T // CHUNK):
             raw = keep.tile([P, 4, CHUNK], F32, name=f"raw{c}")
             nc.sync.dma_start(out=raw[:], in_=xT[:, c * CHUNK : (c + 1) * CHUNK].rearrange("(p j) w -> p j w", j=4))
             raws.append(raw)
-            if c == 0:
-                nc.sync.dma_start(offs_sb[:], offs)
-                nc.sync.dma_start(out=gate_sb[:, :, :EARLY_GATE], in_=gate_rows[:, :, :EARLY_GATE])
+        nc.sync.dma_start(offs_sb[:], offs)
 
-        nc.vector.memset(warm[:], 0.0)
-        nc.scalar.activation(warm[:], warm[:], SILU)
+        nc.vector.memset(table_warm[:], 0.0)
+        nc.scalar.activation(table_warm[:], table_warm[:], SILU)
         nc.gpsimd.memset(w1_planes[2][:].bitcast(I32), 0)
         nc.vector.memset(w1_planes[0][:].bitcast(I32), 0)
         nc.vector.memset(w1_planes[1][:].bitcast(I32), 0)
@@ -95,7 +95,8 @@ def tile_moe_pln_mlp_silu_kernel(
         load_scales(w1_scales_of, w1_planes[0], w1_scales, *SCALE_GROUPS[0])
         load_words(w1_of, w1_words, 2, 4, 1)
         load_scales(w1_scales_of, w1_planes[1], w1_scales, *SCALE_GROUPS[1])
-        load_words(w1_of, w1_words, 4, 8, 1)
+        load_words(w1_of, w1_words, 4, 6, 1)
+        load_words(w1_of, w1_words, 6, 8, 1)
         load_scales(w1_scales_of, w1_planes[2], w1_scales, *SCALE_GROUPS[2])
         load_words(w1_of, w1_words, 8, 12, 1)
         load_words(w1_of, w1_words, 12, 16, 1)
@@ -103,25 +104,28 @@ def tile_moe_pln_mlp_silu_kernel(
         load_words(w2_of, w2_words, 0, E, 2)
         nc.sync.dma_start(pos_sb[0][:], pos1)
         nc.sync.dma_start(pos_sb[1][:], pos2)
-        nc.sync.dma_start(out=gate_sb[:, :, EARLY_GATE:], in_=gate_rows[:, :, EARLY_GATE:])
+        nc.sync.dma_start(out=gate_sb[:, 1, :EARLY_GATE], in_=gate[1, :, :EARLY_GATE])
+        nc.sync.dma_start(out=gate_sb[:, :, EARLY_GATE:], in_=gate[:, :, EARLY_GATE:].rearrange("r p t -> p r t"))
 
         spare = keep.tile([P, 4 * WARM_COLUMNS // EARLY_GATE, EARLY_GATE], BF16, name="spare", align_bytes=64)
         spare_words = keep.tile([P, WARM_COLUMNS], U32, name="spare_words", align_bytes=64)
         spare_scales = keep.tile([P, WARM_COLUMNS], U8, name="spare_scales", align_bytes=64)
         nc.scalar.copy(out=spare[:], in_=gate_sb[:, 0:1, :EARLY_GATE].to_broadcast(list(spare.shape)))
-        nc.vector.quantize_mx(
-            out=spare_words[:].bitcast(FP8X4), scales=spare_scales[:], in_=spare[:].rearrange("p a b -> p (a b)")
-        )
-        for rep in range(4):
-            nc.tensor.matmul_mx(
-                out=banks[7][:, :WARM_COLUMNS],
-                lhsT=w1_of[0][:, : 2 * P].bitcast(FP4X4),
-                lhsT_scale=spare_scales[:, :P],
-                rhs=spare_words[:].bitcast(FP8X4),
-                rhs_scale=spare_scales[:],
-                start=True,
-                stop=True,
+
+        def early_warm_up():
+            nc.vector.quantize_mx(
+                out=spare_words[:].bitcast(FP8X4), scales=spare_scales[:], in_=spare[:].rearrange("p a b -> p (a b)")
             )
+            for warm_pass in range(WARM_PASSES):
+                nc.tensor.matmul_mx(
+                    out=banks[HALF - 1][:, :WARM_COLUMNS],
+                    lhsT=w1_of[0][:, : 2 * P].bitcast(FP4X4),
+                    lhsT_scale=spare_scales[:, :P],
+                    rhs=spare_words[:].bitcast(FP8X4),
+                    rhs_scale=spare_scales[:],
+                    start=True,
+                    stop=True,
+                )
 
         for c, raw in enumerate(raws):
             grouped = keep.tile([P, CHUNK, 4], BF16, name=f"grouped{c}", align_bytes=64)
@@ -140,6 +144,8 @@ def tile_moe_pln_mlp_silu_kernel(
                     scales=x_scales[:, tokens],
                     in_=grouped[:, q0 : q0 + step, :].rearrange("p w j -> p (w j)"),
                 )
+            if c == 0:
+                early_warm_up()
 
         tokens_of, h_of, turned_of, woven_of, codes_of = {}, {}, {}, {}, {}
 
@@ -224,41 +230,50 @@ def tile_moe_pln_mlp_silu_kernel(
         for e0, e1 in GATHERS:
             gather(e0, e1)
 
-        first_bank = [0, 1, 2, 3, 4, 5, 6, 7, 0, 1, 2, 3, 5, 6, 7, 0]
-        turn_bank = [5, 6, 4, 7, 1, 3, 6, 4]
-        for e in range(8):
+        first_bank = list(range(HALF))
+        turn_bank = {0: 5, 1: 6, 3: 4, 2: 7}
+        for e in range(HALF):
             first_layer(e, first_bank[e])
-        for pair in range(4):
+        for pair in turn_bank:
             turn(pair, turn_bank[pair])
-        weave(0, "scalar")
-        weave(1, "scalar")
-        weave(3, "scalar")
+        for pair in (0, 1, 3):
+            weave(pair, "scalar")
         weave(2, "vector")
         quantise(0)
-        for e in range(8, E):
+
+        first_bank.extend([0, 1, 2, 3] + [turn_bank[pair] for pair in (0, 1, 3)] + [0])
+        for pair in (4, 5, 6):
+            turn_bank[pair] = first_bank[2 * pair + 1]
+        turn_bank[7] = turn_bank[2]
+        for e in range(HALF, 13):
             first_layer(e, first_bank[e])
-            if e == 12:
-                turn(4, turn_bank[4])
-                weave(4, "vector")
-                quantise(1)
-            if e == 14:
-                turn(5, turn_bank[5])
-                weave(5, "vector")
+        turn(4, turn_bank[4])
+        weave(4, "vector")
+        quantise(1)
+        first_layer(13, first_bank[13])
+        first_layer(14, first_bank[14])
+        turn(5, turn_bank[5])
+        weave(5, "vector")
+        first_layer(15, first_bank[15])
         turn(6, turn_bank[6])
         turn(7, turn_bank[7])
         weave(6, "scalar")
         weave(7, "scalar")
-        quantise(2)
-        first_product(E - 1, first_bank[12])
+
+        def late_warm_up(bank):
+            first_product(E - 1, bank)
+
+        late_warm_up(first_bank[12])
         second_layer(0, first_bank[12], "vector")
+        quantise(2)
         quantise(3)
         quantise(4)
-        first_product(E - 1, first_bank[14])
+        late_warm_up(first_bank[14])
         second_layer(1, first_bank[14], "scalar")
-        first_product(E - 1, first_bank[15])
+        late_warm_up(first_bank[15])
         second_layer(2, first_bank[15], "scalar")
-        second_layer(3, turn_bank[4], "scalar")
-        second_layer(4, turn_bank[5], "vector")
+        second_layer(3, turn_bank[4], "vector")
+        second_layer(4, turn_bank[5], "scalar")
 
         def fetch(r, t0, w):
             gated = keep.tile([P, w], F32, name=f"gated{r}_{t0}")

@@ -112,7 +112,7 @@ def tile_moe_pln_mlp_silu_kernel(
         spare_scales = keep.tile([P, WARM_COLUMNS], U8, name="spare_scales", align_bytes=64)
         nc.scalar.copy(out=spare[:], in_=gate_sb[:, 0:1, :EARLY_GATE].to_broadcast(list(spare.shape)))
 
-        def early_warm_up():
+        def warm_up():
             nc.vector.quantize_mx(
                 out=spare_words[:].bitcast(FP8X4), scales=spare_scales[:], in_=spare[:].rearrange("p a b -> p (a b)")
             )
@@ -145,7 +145,7 @@ def tile_moe_pln_mlp_silu_kernel(
                     in_=grouped[:, q0 : q0 + step, :].rearrange("p w j -> p (w j)"),
                 )
             if c == 0:
-                early_warm_up()
+                warm_up()
 
         tokens_of, h_of, turned_of, woven_of, codes_of = {}, {}, {}, {}, {}
 
@@ -160,7 +160,7 @@ def tile_moe_pln_mlp_silu_kernel(
                 slots = slice((e - e0) * C, (e - e0 + 1) * C)
                 tokens_of[e] = g_words[:, slots], g_scales[:, slots]
 
-        def first_product(e, bank):
+        def first_layer(e, bank):
             words, scales = tokens_of[e]
             nc.tensor.matmul_mx(
                 out=banks[bank][:],
@@ -171,9 +171,6 @@ def tile_moe_pln_mlp_silu_kernel(
                 start=True,
                 stop=True,
             )
-
-        def first_layer(e, bank):
-            first_product(e, bank)
             h_sb = keep.tile([P, 2, P, 2], BF16, name=f"h_sb{e}", align_bytes=64)
             nc.scalar.activation(h_sb[:], banks[bank][:].rearrange("s (p v d) -> s v p d", v=2, d=2), SILU)
             h_of[e] = h_sb
@@ -260,17 +257,11 @@ def tile_moe_pln_mlp_silu_kernel(
         weave(6, "scalar")
         weave(7, "scalar")
 
-        def late_warm_up(bank):
-            first_product(E - 1, bank)
-
-        late_warm_up(first_bank[12])
         second_layer(0, first_bank[12], "vector")
         quantise(2)
         quantise(3)
         quantise(4)
-        late_warm_up(first_bank[14])
         second_layer(1, first_bank[14], "scalar")
-        late_warm_up(first_bank[15])
         second_layer(2, first_bank[15], "scalar")
         second_layer(3, turn_bank[4], "vector")
         second_layer(4, turn_bank[5], "scalar")

@@ -17,6 +17,7 @@ U8 = mybir.dt.uint8
 FP8X4 = mybir.dt.float8_e4m3fn_x4
 FP4X4 = mybir.dt.float4_e2m1fn_x4
 SILU = mybir.ActivationFunctionType.Silu
+COPY = mybir.ActivationFunctionType.Copy
 MULT = mybir.AluOpType.mult
 ADD = mybir.AluOpType.add
 
@@ -29,8 +30,7 @@ SCALE_GROUPS = [(0, 4), (4, 8), (8, 16)]
 WARM_PASSES = 4
 WARM_COLUMNS = 256
 EARLY_GATE = 32
-ADDED_ON_TENSOR = 512
-ADDED_ON_VECTOR = [256, 128, 128]
+PIECES = [(288, 1), (288, 1), (256, 2), (128, 2), (64, 2)]
 
 
 def tile_moe_pln_mlp_silu_kernel(
@@ -266,40 +266,42 @@ def tile_moe_pln_mlp_silu_kernel(
         second_layer(3, turn_bank[4], "vector")
         second_layer(4, turn_bank[5], "scalar")
 
-        def fetch(r, t0, w):
-            gated = keep.tile([P, w], F32, name=f"gated{r}_{t0}")
-            entries = pos_sb[r][:, t0 // 16 : (t0 + w) // 16]
-            nc.vector.tensor_tensor(gated[:], y_sb[:].indirect(entries), gate_sb[:, r, t0 : t0 + w], MULT)
-            return gated
+        def entries(r, t0, w):
+            return pos_sb[r][:, t0 // 16 : (t0 + w) // 16]
 
-        blocks = [slice(b * P, (b + 1) * P) for b in range(ADDED_ON_TENSOR // P)]
-        first_choice = fetch(0, 0, ADDED_ON_TENSOR)
-        widths = [min(2 * P, ADDED_ON_TENSOR - t0) for t0 in range(0, ADDED_ON_TENSOR, 2 * P)]
-        second_choice = [fetch(1, 2 * P * k, w) for k, w in enumerate(widths)]
-        for b, cols in enumerate(blocks):
-            nc.tensor.matmul(banks[b][:, :P], first_choice[:, cols], ident[:], start=True, stop=False, is_transpose=True)
-        for b in range(len(blocks)):
-            nc.tensor.matmul(
-                banks[b][:, :P], second_choice[b // 2][:, blocks[b % 2]], ident[:], start=False, stop=True, is_transpose=True
-            )
-        sums = keep.tile([P, ADDED_ON_TENSOR], F32, name="sums")
-        back_banks = banks[len(blocks) :]
-        for b, cols in enumerate(blocks):
-            nc.scalar.copy(out=sums[:, cols], in_=banks[b][:, :P])
-            nc.tensor.transpose(back_banks[b // 2][:, blocks[b % 2]], sums[:, cols], ident[:])
-        for k, w in enumerate(widths):
-            result = keep.tile([P, w], F32, name=f"result_turned{k}")
-            nc.scalar.copy(out=result[:], in_=back_banks[k][:, :w])
-            nc.scalar.dma_start(out=out[:, 2 * P * k : 2 * P * k + w], in_=result[:])
+        pieces = []
+        t0 = 0
+        for w, on_scalar in PIECES:
+            fetched = keep.tile([P, on_scalar, w], F32, name=f"fetched{t0}")
+            gated = keep.tile([P, on_scalar, w], F32, name=f"gated{t0}")
+            for r in range(2 - on_scalar, 2):
+                nc.scalar.activation(fetched[:, r - 2 + on_scalar, :], y_sb[:].indirect(entries(r, t0, w)), COPY)
+            pieces.append((t0, w, on_scalar, fetched, gated))
+            t0 = t0 + w
 
-        starts = [ADDED_ON_TENSOR + sum(ADDED_ON_VECTOR[:k]) for k in range(len(ADDED_ON_VECTOR))]
-        first_choice = fetch(0, ADDED_ON_TENSOR, T - ADDED_ON_TENSOR)
-        second_choice = [fetch(1, starts[0], ADDED_ON_VECTOR[0])]
-        for k, (t0, w) in enumerate(zip(starts, ADDED_ON_VECTOR)):
-            if k + 1 < len(starts):
-                second_choice.append(fetch(1, starts[k + 1], ADDED_ON_VECTOR[k + 1]))
+        shared = sum(w for w, on_scalar in PIECES if on_scalar == 1)
+        first_gated = keep.tile([P, shared], F32, name="first_gated")
+
+        def gate_fetched(k):
+            t0, w, on_scalar, fetched, gated = pieces[k]
+            r0 = 2 - on_scalar
+            nc.vector.tensor_tensor(gated[:], fetched[:], gate_sb[:, r0:, t0 : t0 + w], MULT)
+
+        def add_and_store(k):
+            t0, w, on_scalar, fetched, gated = pieces[k]
             result = keep.tile([P, w], F32, name=f"result{t0}")
-            cols = slice(t0 - ADDED_ON_TENSOR, t0 - ADDED_ON_TENSOR + w)
-            nc.vector.tensor_tensor(result[:], first_choice[:, cols], second_choice[k][:], ADD)
-            queue = nc.scalar if k + 1 == len(starts) else nc.sync
+            first = gated[:, 0, :] if on_scalar == 2 else first_gated[:, t0 : t0 + w]
+            nc.vector.tensor_tensor(result[:], first, gated[:, on_scalar - 1, :], ADD)
+            queue = nc.scalar if k + 1 == len(pieces) else nc.sync
             queue.dma_start(out=out[:, t0 : t0 + w], in_=result[:])
+
+        nc.vector.tensor_tensor(first_gated[:], y_sb[:].indirect(entries(0, 0, shared)), gate_sb[:, 0, :shared], MULT)
+        gate_fetched(0)
+        gate_fetched(1)
+        add_and_store(0)
+        add_and_store(1)
+        gate_fetched(2)
+        for k in range(3, len(pieces)):
+            gate_fetched(k)
+            add_and_store(k - 1)
+        add_and_store(len(pieces) - 1)

@@ -107,26 +107,6 @@ def tile_moe_pln_mlp_silu_kernel(
         nc.sync.dma_start(out=gate_sb[:, 1, :EARLY_GATE], in_=gate[1, :, :EARLY_GATE])
         nc.sync.dma_start(out=gate_sb[:, :, EARLY_GATE:], in_=gate[:, :, EARLY_GATE:].rearrange("r p t -> p r t"))
 
-        spare = keep.tile([P, 4 * WARM_COLUMNS // EARLY_GATE, EARLY_GATE], BF16, name="spare", align_bytes=64)
-        spare_words = keep.tile([P, WARM_COLUMNS], U32, name="spare_words", align_bytes=64)
-        spare_scales = keep.tile([P, WARM_COLUMNS], U8, name="spare_scales", align_bytes=64)
-        nc.scalar.copy(out=spare[:], in_=gate_sb[:, 0:1, :EARLY_GATE].to_broadcast(list(spare.shape)))
-
-        def warm_up():
-            nc.vector.quantize_mx(
-                out=spare_words[:].bitcast(FP8X4), scales=spare_scales[:], in_=spare[:].rearrange("p a b -> p (a b)")
-            )
-            for warm_pass in range(WARM_PASSES):
-                nc.tensor.matmul_mx(
-                    out=banks[HALF - 1][:, :WARM_COLUMNS],
-                    lhsT=w1_of[0][:, : 2 * P].bitcast(FP4X4),
-                    lhsT_scale=spare_scales[:, :P],
-                    rhs=spare_words[:].bitcast(FP8X4),
-                    rhs_scale=spare_scales[:],
-                    start=True,
-                    stop=True,
-                )
-
         for c, raw in enumerate(raws):
             grouped = keep.tile([P, CHUNK, 4], BF16, name=f"grouped{c}", align_bytes=64)
             src = raw[:].rearrange("p j (g i) -> p g j i", i=4)
@@ -144,8 +124,6 @@ def tile_moe_pln_mlp_silu_kernel(
                     scales=x_scales[:, tokens],
                     in_=grouped[:, q0 : q0 + step, :].rearrange("p w j -> p (w j)"),
                 )
-            if c == 0:
-                warm_up()
 
         tokens_of, h_of, turned_of, woven_of, codes_of = {}, {}, {}, {}, {}
 

@@ -23,14 +23,13 @@ ADD = mybir.AluOpType.add
 
 CHUNK = 256
 CHUNK_ON_VECTOR = 160
+EARLY_GATE = 32
 HALF = E // 2
 GATHERS = [(e, e + 1) for e in range(HALF)] + [(e, e + 2) for e in range(HALF, E, 2)]
 QUANTISE = [(0, 4), (4, 8), (8, 12), (12, 14), (14, 16)]
 SCALE_GROUPS = [(0, 4), (4, 8), (8, 16)]
-WARM_PASSES = 4
-WARM_COLUMNS = 256
-EARLY_GATE = 32
-PIECES = [(288, 1), (288, 1), (256, 2), (128, 2), (64, 2)]
+SHARED_PIECES = [288, 288]
+SCALAR_PIECES = [256, 128, 64]
 
 
 def tile_moe_pln_mlp_silu_kernel(
@@ -111,18 +110,18 @@ def tile_moe_pln_mlp_silu_kernel(
             grouped = keep.tile([P, CHUNK, 4], BF16, name=f"grouped{c}", align_bytes=64)
             src = raw[:].rearrange("p j (g i) -> p g j i", i=4)
             dst = grouped[:].rearrange("p (g i) j -> p g j i", i=4)
+            part = CHUNK // 2 if c == len(raws) - 1 else CHUNK
             cut = CHUNK_ON_VECTOR // 4
-            halves = 2 if c == len(raws) - 1 else 1
-            step = CHUNK // halves
-            for g0, g1 in ((0, step // 4), (step // 4, cut)) if halves == 2 else ((0, cut),):
+            for g0 in range(0, cut, part // 4):
+                g1 = min(g0 + part // 4, cut)
                 nc.vector.tensor_copy(out=dst[:, g0:g1], in_=src[:, g0:g1])
             nc.scalar.copy(out=dst[:, cut:], in_=src[:, cut:])
-            for q0 in range(0, CHUNK, step):
-                tokens = slice(c * CHUNK + q0, c * CHUNK + q0 + step)
+            for t0 in range(0, CHUNK, part):
+                tokens = slice(c * CHUNK + t0, c * CHUNK + t0 + part)
                 nc.vector.quantize_mx(
                     out=x_words[:, tokens].bitcast(FP8X4),
                     scales=x_scales[:, tokens],
-                    in_=grouped[:, q0 : q0 + step, :].rearrange("p w j -> p (w j)"),
+                    in_=grouped[:, t0 : t0 + part, :].rearrange("p w j -> p (w j)"),
                 )
 
         tokens_of, h_of, turned_of, woven_of, codes_of = {}, {}, {}, {}, {}
@@ -206,7 +205,7 @@ def tile_moe_pln_mlp_silu_kernel(
             gather(e0, e1)
 
         first_bank = list(range(HALF))
-        turn_bank = {0: 5, 1: 6, 3: 4, 2: 7}
+        turn_bank = {pair: HALF // 2 + pair for pair in range(HALF // 2)}
         for e in range(HALF):
             first_layer(e, first_bank[e])
         for pair in turn_bank:
@@ -244,42 +243,41 @@ def tile_moe_pln_mlp_silu_kernel(
         second_layer(3, turn_bank[4], "vector")
         second_layer(4, turn_bank[5], "scalar")
 
-        def entries(r, t0, w):
-            return pos_sb[r][:, t0 // 16 : (t0 + w) // 16]
+        def slots_of(choice, t0, w):
+            return y_sb[:].indirect(pos_sb[choice][:, t0 // 16 : (t0 + w) // 16])
 
-        pieces = []
-        t0 = 0
-        for w, on_scalar in PIECES:
-            fetched = keep.tile([P, on_scalar, w], F32, name=f"fetched{t0}")
-            gated = keep.tile([P, on_scalar, w], F32, name=f"gated{t0}")
-            for r in range(2 - on_scalar, 2):
-                nc.scalar.activation(fetched[:, r - 2 + on_scalar, :], y_sb[:].indirect(entries(r, t0, w)), COPY)
-            pieces.append((t0, w, on_scalar, fetched, gated))
-            t0 = t0 + w
+        widths = SHARED_PIECES + SCALAR_PIECES
+        starts = [sum(widths[:k]) for k in range(len(widths))]
+        scalar_from = [1] * len(SHARED_PIECES) + [0] * len(SCALAR_PIECES)
+        fetched, gated = [], []
+        for t0, w, c0 in zip(starts, widths, scalar_from):
+            fetched.append(keep.tile([P, 2 - c0, w], F32, name=f"fetched{t0}"))
+            gated.append(keep.tile([P, 2 - c0, w], F32, name=f"gated{t0}"))
+            for choice in range(c0, 2):
+                nc.scalar.activation(fetched[-1][:, choice - c0, :], slots_of(choice, t0, w), COPY)
 
-        shared = sum(w for w, on_scalar in PIECES if on_scalar == 1)
+        shared = sum(SHARED_PIECES)
         first_gated = keep.tile([P, shared], F32, name="first_gated")
 
-        def gate_fetched(k):
-            t0, w, on_scalar, fetched, gated = pieces[k]
-            r0 = 2 - on_scalar
-            nc.vector.tensor_tensor(gated[:], fetched[:], gate_sb[:, r0:, t0 : t0 + w], MULT)
+        def apply_gate(k):
+            t0, w, c0 = starts[k], widths[k], scalar_from[k]
+            nc.vector.tensor_tensor(gated[k][:], fetched[k][:], gate_sb[:, c0:, t0 : t0 + w], MULT)
 
         def add_and_store(k):
-            t0, w, on_scalar, fetched, gated = pieces[k]
+            t0, w, c0 = starts[k], widths[k], scalar_from[k]
             result = keep.tile([P, w], F32, name=f"result{t0}")
-            first = gated[:, 0, :] if on_scalar == 2 else first_gated[:, t0 : t0 + w]
-            nc.vector.tensor_tensor(result[:], first, gated[:, on_scalar - 1, :], ADD)
-            queue = nc.scalar if k + 1 == len(pieces) else nc.sync
+            first = first_gated[:, t0 : t0 + w] if c0 == 1 else gated[k][:, 0, :]
+            nc.vector.tensor_tensor(result[:], first, gated[k][:, 1 - c0, :], ADD)
+            queue = nc.scalar if k + 1 == len(widths) else nc.sync
             queue.dma_start(out=out[:, t0 : t0 + w], in_=result[:])
 
-        nc.vector.tensor_tensor(first_gated[:], y_sb[:].indirect(entries(0, 0, shared)), gate_sb[:, 0, :shared], MULT)
-        gate_fetched(0)
-        gate_fetched(1)
-        add_and_store(0)
-        add_and_store(1)
-        gate_fetched(2)
-        for k in range(3, len(pieces)):
-            gate_fetched(k)
+        nc.vector.tensor_tensor(first_gated[:], slots_of(0, 0, shared), gate_sb[:, 0, :shared], MULT)
+        for k in range(len(SHARED_PIECES)):
+            apply_gate(k)
+        for k in range(len(SHARED_PIECES)):
+            add_and_store(k)
+        apply_gate(len(SHARED_PIECES))
+        for k in range(len(SHARED_PIECES) + 1, len(widths)):
+            apply_gate(k)
             add_and_store(k - 1)
-        add_and_store(len(pieces) - 1)
+        add_and_store(len(widths) - 1)

@@ -27,6 +27,7 @@ EARLY_GATE = 32
 HALF = E // 2
 GATHERS = [(e, e + 1) for e in range(HALF)] + [(e, e + 2) for e in range(HALF, E, 2)]
 QUANTISE = [(0, 4), (4, 8), (8, 12), (12, 14), (14, 16)]
+FIRST_SORTED = 12
 SCALE_GROUPS = [(0, 4), (4, 8), (8, 16)]
 SHARED_PIECES = [288, 288]
 SCALAR_PIECES = [256, 128, 64]
@@ -93,12 +94,16 @@ def tile_moe_pln_mlp_silu_kernel(
         load_words(w1_of, w1_words, 1, 2, 1)
         load_scales(w1_scales_of, w1_planes[0], w1_scales, *SCALE_GROUPS[0])
         load_words(w1_of, w1_words, 2, 4, 1)
+        load_words(w1_of, w1_words, 12, 13, 1)
         load_scales(w1_scales_of, w1_planes[1], w1_scales, *SCALE_GROUPS[1])
         load_words(w1_of, w1_words, 4, 6, 1)
+        load_words(w1_of, w1_words, 13, 14, 1)
         load_words(w1_of, w1_words, 6, 8, 1)
+        load_words(w1_of, w1_words, 14, 15, 1)
         load_scales(w1_scales_of, w1_planes[2], w1_scales, *SCALE_GROUPS[2])
-        load_words(w1_of, w1_words, 8, 12, 1)
-        load_words(w1_of, w1_words, 12, 16, 1)
+        load_words(w1_of, w1_words, 15, 16, 1)
+        load_words(w1_of, w1_words, 8, 10, 1)
+        load_words(w1_of, w1_words, 10, 12, 1)
         load_scales(w2_scales_of, w2_plane, w2_scales, 0, E)
         load_words(w2_of, w2_words, 0, E, 2)
         nc.sync.dma_start(pos_sb[0][:], pos1)
@@ -152,6 +157,38 @@ def tile_moe_pln_mlp_silu_kernel(
             nc.scalar.activation(h_sb[:], banks[bank][:].rearrange("s (p v d) -> s v p d", v=2, d=2), SILU)
             h_of[e] = h_sb
 
+        sorted_words, sorted_scales = {}, {}
+
+        def sort_words(e):
+            tile = keep.tile([P, 4, P, 2], U8, name=f"sorted_words{e}", align_bytes=64)
+            nc.gpsimd.tensor_copy(out=tile[:], in_=w1_of[e].rearrange("p (m j b) -> p j m b", j=4, b=2))
+            sorted_words[e] = tile
+
+        def sort_scales():
+            n = E - FIRST_SORTED
+            tile = keep.tile([P, n, 4, P], U8, name="sorted_scales", align_bytes=64)
+            first = (FIRST_SORTED - SCALE_GROUPS[2][0]) * H
+            nc.gpsimd.tensor_copy(out=tile[:], in_=w1_planes[2][:, first:].rearrange("p (e m j) -> p e j m", e=n, j=4))
+            for e in range(FIRST_SORTED, E):
+                sorted_scales[e] = tile[:, e - FIRST_SORTED]
+
+        def sorted_first_layer(e, bank):
+            words, scales = tokens_of[e]
+            for j in range(4):
+                nc.tensor.matmul_mx(
+                    out=banks[bank][:, j * C : (j + 1) * C],
+                    lhsT=sorted_words[e][:, j].rearrange("p m b -> p (m b)").bitcast(FP4X4),
+                    lhsT_scale=sorted_scales[e][:, j],
+                    rhs=words.bitcast(FP8X4),
+                    rhs_scale=scales,
+                    start=True,
+                    stop=True,
+                )
+            woven, slot0 = woven_of[e // 2]
+            slot0 = slot0 + (e % 2) * C
+            dst = woven[:, 4 * slot0 : 4 * (slot0 + C)].rearrange("p (s j) -> p s j", j=4)
+            nc.scalar.activation(dst, banks[bank][:].rearrange("p (j s) -> p s j", j=4), SILU)
+
         def turn(pair, bank):
             turned = banks[bank][:].rearrange("p (v s) -> p v s", v=2)
             for half, e in enumerate((2 * pair, 2 * pair + 1)):
@@ -204,44 +241,39 @@ def tile_moe_pln_mlp_silu_kernel(
         for e0, e1 in GATHERS:
             gather(e0, e1)
 
-        first_bank = list(range(HALF))
-        turn_bank = {pair: HALF // 2 + pair for pair in range(HALF // 2)}
+        for e in range(FIRST_SORTED, E):
+            sort_words(e)
+        sort_scales()
+
         for e in range(HALF):
-            first_layer(e, first_bank[e])
-        for pair in turn_bank:
-            turn(pair, turn_bank[pair])
-        for pair in (0, 1, 3):
-            weave(pair, "scalar")
+            first_layer(e, e)
+        for pair in range(3):
+            turn(pair, 4 + pair)
+        weave(0, "scalar")
+        weave(1, "scalar")
+        for e in range(8, 12):
+            first_layer(e, e - 8)
         weave(2, "vector")
         quantise(0)
-
-        first_bank.extend([0, 1, 2, 3] + [turn_bank[pair] for pair in (0, 1, 3)] + [0])
-        for pair in (4, 5, 6):
-            turn_bank[pair] = first_bank[2 * pair + 1]
-        turn_bank[7] = turn_bank[2]
-        for e in range(HALF, 13):
-            first_layer(e, first_bank[e])
-        turn(4, turn_bank[4])
-        weave(4, "vector")
-        quantise(1)
-        first_layer(13, first_bank[13])
-        first_layer(14, first_bank[14])
-        turn(5, turn_bank[5])
+        turn(3, 0)
+        turn(4, 1)
+        weave(3, "scalar")
+        weave(4, "scalar")
+        turn(5, 3)
         weave(5, "vector")
-        first_layer(15, first_bank[15])
-        turn(6, turn_bank[6])
-        turn(7, turn_bank[7])
-        weave(6, "scalar")
-        weave(7, "scalar")
-
-        second_layer(0, first_bank[12], "vector")
+        sorted_first_layer(12, 7)
+        sorted_first_layer(13, 4)
+        sorted_first_layer(14, 5)
+        sorted_first_layer(15, 6)
+        quantise(1)
+        second_layer(0, 7, "vector")
         quantise(2)
         quantise(3)
         quantise(4)
-        second_layer(1, first_bank[14], "scalar")
-        second_layer(2, first_bank[15], "scalar")
-        second_layer(3, turn_bank[4], "vector")
-        second_layer(4, turn_bank[5], "scalar")
+        second_layer(1, 2, "scalar")
+        second_layer(2, 0, "scalar")
+        second_layer(3, 1, "scalar")
+        second_layer(4, 3, "vector")
 
         def slots_of(choice, t0, w):
             return y_sb[:].indirect(pos_sb[choice][:, t0 // 16 : (t0 + w) // 16])

@@ -300,7 +300,7 @@ def tile_moe_pln_mlp_silu_kernel(
             result = keep.tile([P, w], F32, name=f"result{t0}")
             first = first_gated[:, t0 : t0 + w] if c0 == 1 else gated[k][:, 0, :]
             nc.vector.tensor_tensor(result[:], first, gated[k][:, 1 - c0, :], ADD)
-            queue = nc.scalar if k + 1 == len(widths) else nc.sync
+            queue = nc.scalar if k >= len(SHARED_PIECES) else nc.sync
             queue.dma_start(out=out[:, t0 : t0 + w], in_=result[:])
 
         nc.vector.tensor_tensor(first_gated[:], slots_of(0, 0, shared), gate_sb[:, 0, :shared], MULT)

@@ -21,8 +21,7 @@ COPY = mybir.ActivationFunctionType.Copy
 MULT = mybir.AluOpType.mult
 ADD = mybir.AluOpType.add
 
-CHUNK = 256
-CHUNK_ON_VECTOR = 160
+CHUNKS = [(512, 256), (256, 160), (256, 160)]
 EARLY_GATE = 32
 HALF = E // 2
 GATHERS = [(e, e + 1) for e in range(HALF)] + [(e, e + 2) for e in range(HALF, E, 2)]
@@ -56,11 +55,15 @@ def tile_moe_pln_mlp_silu_kernel(
         banks = [psum.tile([P, H], F32, name=f"bank{b}") for b in range(8)]
 
         nc.sync.dma_start(out=gate_sb[:, 0, :EARLY_GATE], in_=gate[0, :, :EARLY_GATE])
-        raws = []
-        for c in range(T // CHUNK):
-            raw = keep.tile([P, 4, CHUNK], F32, name=f"raw{c}")
-            nc.sync.dma_start(out=raw[:], in_=xT[:, c * CHUNK : (c + 1) * CHUNK].rearrange("(p j) w -> p j w", j=4))
-            raws.append(raw)
+        raws, t0 = [], 0
+        for c, (w, on_vector) in enumerate(CHUNKS):
+            raw = keep.tile([P, 4, w], F32, name=f"raw{c}")
+            rows = xT[:, t0 : t0 + w].rearrange("(p j) w -> p j w", j=4)
+            step = 2 if c == 0 else 4
+            for j in range(0, 4, step):
+                nc.sync.dma_start(out=raw[:, j : j + step], in_=rows[:, j : j + step])
+            raws.append((raw, t0, w, on_vector))
+            t0 = t0 + w
         nc.sync.dma_start(offs_sb[:], offs)
 
         nc.vector.memset(table_warm[:], 0.0)
@@ -111,18 +114,18 @@ def tile_moe_pln_mlp_silu_kernel(
         nc.sync.dma_start(out=gate_sb[:, 1, :EARLY_GATE], in_=gate[1, :, :EARLY_GATE])
         nc.sync.dma_start(out=gate_sb[:, :, EARLY_GATE:], in_=gate[:, :, EARLY_GATE:].rearrange("r p t -> p r t"))
 
-        for c, raw in enumerate(raws):
-            grouped = keep.tile([P, CHUNK, 4], BF16, name=f"grouped{c}", align_bytes=64)
+        for c, (raw, first, width, on_vector) in enumerate(raws):
+            grouped = keep.tile([P, width, 4], BF16, name=f"grouped{c}", align_bytes=64)
             src = raw[:].rearrange("p j (g i) -> p g j i", i=4)
             dst = grouped[:].rearrange("p (g i) j -> p g j i", i=4)
-            part = CHUNK // 2 if c == len(raws) - 1 else CHUNK
-            cut = CHUNK_ON_VECTOR // 4
+            part = width if c == 1 else width // 2
+            cut = on_vector // 4
             for g0 in range(0, cut, part // 4):
                 g1 = min(g0 + part // 4, cut)
                 nc.vector.tensor_copy(out=dst[:, g0:g1], in_=src[:, g0:g1])
             nc.scalar.copy(out=dst[:, cut:], in_=src[:, cut:])
-            for t0 in range(0, CHUNK, part):
-                tokens = slice(c * CHUNK + t0, c * CHUNK + t0 + part)
+            for t0 in range(0, width, part):
+                tokens = slice(first + t0, first + t0 + part)
                 nc.vector.quantize_mx(
                     out=x_words[:, tokens].bitcast(FP8X4),
                     scales=x_scales[:, tokens],

from contextlib import ExitStack

import concourse.mybir as mybir
from concourse.masks import make_identity

K, T, E, C, H, N = 512, 1024, 16, 128, 512, 128
S = E * C
P = 128
FLOPS = 2 * K * H * S + 2 * H * N * S

F32 = mybir.dt.float32
BF16 = mybir.dt.bfloat16
I32 = mybir.dt.int32
U32 = mybir.dt.uint32
U16 = mybir.dt.uint16
U8 = mybir.dt.uint8
FP8X4 = mybir.dt.float8_e4m3fn_x4
FP4X4 = mybir.dt.float4_e2m1fn_x4
SILU = mybir.ActivationFunctionType.Silu
COPY = mybir.ActivationFunctionType.Copy
MULT = mybir.AluOpType.mult
ADD = mybir.AluOpType.add

CHUNKS = [(512, 256), (256, 160), (256, 160)]
EARLY_GATE = 32
HALF = E // 2
GATHERS = [(e, e + 1) for e in range(HALF)] + [(e, e + 2) for e in range(HALF, E, 2)]
QUANTISE = [(0, 4), (4, 8), (8, 12), (12, 14), (14, 16)]
FIRST_SORTED = 12
SCALE_GROUPS = [(0, 4), (4, 8), (8, 16)]
SHARED_PIECES = [288, 288]
SCALAR_PIECES = [256, 128, 64]


def tile_moe_pln_mlp_silu_kernel(
    tc, xT, w1_words, w1_scales, w2_words, w2_scales, gate, offs, pos1, pos2, out
):
    nc = tc.nc
    with ExitStack() as ctx:
        lists = ctx.enter_context(tc.tile_pool(name="lists", bufs=1))
        keep = ctx.enter_context(tc.tile_pool(name="keep", bufs=1))
        psum = ctx.enter_context(tc.psum_pool(name="psum", bufs=1))

        offs_sb = lists.tile([P, S // 16], U16, name="offs_sb")
        pos_sb = [lists.tile([P, T // 16], U16, name=f"pos{r}_sb") for r in (1, 2)]

        x_words = keep.tile([P, T], U32, name="x_words", align_bytes=64)
        x_scales = keep.tile([P, T], U8, name="x_scales", align_bytes=64)
        w1_planes = [keep.tile([P, (e1 - e0) * H], U8, name=f"w1_plane{e0}", align_bytes=64) for e0, e1 in SCALE_GROUPS]
        w2_plane = keep.tile([P, E * N], U8, name="w2_plane", align_bytes=64)
        gate_sb = keep.tile([P, 2, T], F32, name="gate_sb")
        y_sb = keep.tile([P, S], F32, name="y_sb")
        ident = keep.tile([P, P], F32, name="ident")
        table_warm = keep.tile([P, 1], F32, name="table_warm")
        banks = [psum.tile([P, H], F32, name=f"bank{b}") for b in range(8)]

        nc.sync.dma_start(out=gate_sb[:, 0, :EARLY_GATE], in_=gate[0, :, :EARLY_GATE])
        raws, t0 = [], 0
        for c, (w, on_vector) in enumerate(CHUNKS):
            raw = keep.tile([P, 4, w], F32, name=f"raw{c}")
            rows = xT[:, t0 : t0 + w].rearrange("(p j) w -> p j w", j=4)
            step = 2 if c == 0 else 4
            for j in range(0, 4, step):
                nc.sync.dma_start(out=raw[:, j : j + step], in_=rows[:, j : j + step])
            raws.append((raw, t0, w, on_vector))
            t0 = t0 + w
        nc.sync.dma_start(offs_sb[:], offs)

        nc.vector.memset(table_warm[:], 0.0)
        nc.scalar.activation(table_warm[:], table_warm[:], SILU)
        nc.gpsimd.memset(w1_planes[2][:].bitcast(I32), 0)
        nc.vector.memset(w1_planes[0][:].bitcast(I32), 0)
        nc.vector.memset(w1_planes[1][:].bitcast(I32), 0)
        nc.vector.memset(w2_plane[:].bitcast(I32), 0)
        nc.vector.memset(x_scales[:].bitcast(I32), 0)
        make_identity(nc, ident[:])

        w1_of, w1_scales_of, w2_of, w2_scales_of = {}, {}, {}, {}

        def load_scales(views, plane, src, e0, e1):
            rows = plane[:].rearrange("p (e i) -> p e i", e=e1 - e0)
            for r in range(4):
                nc.sync.dma_start(
                    out=rows[r:P:32].bitcast(I32),
                    in_=src[e0:e1, 0, r:16:4, :].rearrange("e q i -> q e i").bitcast(I32),
                )
            for e in range(e0, e1):
                views[e] = rows[:, e - e0, :]

        def load_words(views, src, e0, e1, layer):
            words = keep.tile([P, e1 - e0, src.shape[3]], U8, name=f"w{layer}_words{e0}", align_bytes=64)
            nc.sync.dma_start(out=words[:].bitcast(I32), in_=src[e0:e1, 0].rearrange("e p b -> p e b").bitcast(I32))
            for e in range(e0, e1):
                views[e] = words[:, e - e0, :]

        load_words(w1_of, w1_words, 0, 1, 1)
        load_words(w1_of, w1_words, 1, 2, 1)
        load_scales(w1_scales_of, w1_planes[0], w1_scales, *SCALE_GROUPS[0])
        load_words(w1_of, w1_words, 2, 4, 1)
        load_words(w1_of, w1_words, 12, 13, 1)
        load_scales(w1_scales_of, w1_planes[1], w1_scales, *SCALE_GROUPS[1])
        load_words(w1_of, w1_words, 4, 6, 1)
        load_words(w1_of, w1_words, 13, 14, 1)
        load_words(w1_of, w1_words, 6, 8, 1)
        load_words(w1_of, w1_words, 14, 15, 1)
        load_scales(w1_scales_of, w1_planes[2], w1_scales, *SCALE_GROUPS[2])
        load_words(w1_of, w1_words, 15, 16, 1)
        load_words(w1_of, w1_words, 8, 10, 1)
        load_words(w1_of, w1_words, 10, 12, 1)
        load_scales(w2_scales_of, w2_plane, w2_scales, 0, E)
        load_words(w2_of, w2_words, 0, E, 2)
        nc.sync.dma_start(pos_sb[0][:], pos1)
        nc.sync.dma_start(pos_sb[1][:], pos2)
        nc.sync.dma_start(out=gate_sb[:, 1, :EARLY_GATE], in_=gate[1, :, :EARLY_GATE])
        nc.sync.dma_start(out=gate_sb[:, :, EARLY_GATE:], in_=gate[:, :, EARLY_GATE:].rearrange("r p t -> p r t"))

        for c, (raw, first, width, on_vector) in enumerate(raws):
            grouped = keep.tile([P, width, 4], BF16, name=f"grouped{c}", align_bytes=64)
            src = raw[:].rearrange("p j (g i) -> p g j i", i=4)
            dst = grouped[:].rearrange("p (g i) j -> p g j i", i=4)
            part = width if c == 1 else width // 2
            cut = on_vector // 4
            for g0 in range(0, cut, part // 4):
                g1 = min(g0 + part // 4, cut)
                nc.vector.tensor_copy(out=dst[:, g0:g1], in_=src[:, g0:g1])
            nc.scalar.copy(out=dst[:, cut:], in_=src[:, cut:])
            for t0 in range(0, width, part):
                tokens = slice(first + t0, first + t0 + part)
                nc.vector.quantize_mx(
                    out=x_words[:, tokens].bitcast(FP8X4),
                    scales=x_scales[:, tokens],
                    in_=grouped[:, t0 : t0 + part, :].rearrange("p w j -> p (w j)"),
                )

        tokens_of, h_of, turned_of, woven_of, codes_of = {}, {}, {}, {}, {}

        def gather(e0, e1):
            w = (e1 - e0) * C
            entries = offs_sb[:, e0 * C // 16 : e1 * C // 16]
            g_words = keep.tile([P, w], U32, name=f"g_words{e0}", align_bytes=64)
            g_scales = keep.tile([P, w], U8, name=f"g_scales{e0}", align_bytes=64)
            nc.vector.tensor_copy(out=g_words[:], in_=x_words[:].indirect(entries))
            nc.vector.tensor_copy(out=g_scales[:], in_=x_scales[:].indirect(entries))
            for e in range(e0, e1):
                slots = slice((e - e0) * C, (e - e0 + 1) * C)
                tokens_of[e] = g_words[:, slots], g_scales[:, slots]

        def first_layer(e, bank):
            words, scales = tokens_of[e]
            nc.tensor.matmul_mx(
                out=banks[bank][:],
                lhsT=words.bitcast(FP8X4),
                lhsT_scale=scales,
                rhs=w1_of[e].bitcast(FP4X4),
                rhs_scale=w1_scales_of[e],
                start=True,
                stop=True,
            )
            h_sb = keep.tile([P, 2, P, 2], BF16, name=f"h_sb{e}", align_bytes=64)
            nc.scalar.activation(h_sb[:], banks[bank][:].rearrange("s (p v d) -> s v p d", v=2, d=2), SILU)
            h_of[e] = h_sb

        sorted_words, sorted_scales = {}, {}

        def sort_words(e):
            tile = keep.tile([P, 4, P, 2], U8, name=f"sorted_words{e}", align_bytes=64)
            nc.gpsimd.tensor_copy(out=tile[:], in_=w1_of[e].rearrange("p (m j b) -> p j m b", j=4, b=2))
            sorted_words[e] = tile

        def sort_scales():
            n = E - FIRST_SORTED
            tile = keep.tile([P, n, 4, P], U8, name="sorted_scales", align_bytes=64)
            first = (FIRST_SORTED - SCALE_GROUPS[2][0]) * H
            nc.gpsimd.tensor_copy(out=tile[:], in_=w1_planes[2][:, first:].rearrange("p (e m j) -> p e j m", e=n, j=4))
            for e in range(FIRST_SORTED, E):
                sorted_scales[e] = tile[:, e - FIRST_SORTED]

        def sorted_first_layer(e, bank):
            words, scales = tokens_of[e]
            for j in range(4):
                nc.tensor.matmul_mx(
                    out=banks[bank][:, j * C : (j + 1) * C],
                    lhsT=sorted_words[e][:, j].rearrange("p m b -> p (m b)").bitcast(FP4X4),
                    lhsT_scale=sorted_scales[e][:, j],
                    rhs=words.bitcast(FP8X4),
                    rhs_scale=scales,
                    start=True,
                    stop=True,
                )
            woven, slot0 = woven_of[e // 2]
            slot0 = slot0 + (e % 2) * C
            dst = woven[:, 4 * slot0 : 4 * (slot0 + C)].rearrange("p (s j) -> p s j", j=4)
            nc.scalar.activation(dst, banks[bank][:].rearrange("p (j s) -> p s j", j=4), SILU)

        def turn(pair, bank):
            turned = banks[bank][:].rearrange("p (v s) -> p v s", v=2)
            for half, e in enumerate((2 * pair, 2 * pair + 1)):
                words = h_of[e][:].rearrange("s v p d -> s (v p d)").bitcast(F32)
                for v in range(2):
                    nc.tensor.transpose(turned[:, v, half * C : (half + 1) * C], words[:, v * P : (v + 1) * P], ident[:])
            turned_of[pair] = turned

        for e0, e1 in QUANTISE:
            woven = keep.tile([P, (e1 - e0) * C * 4], BF16, name=f"woven{e0}", align_bytes=64)
            for e in range(e0, e1, 2):
                woven_of[e // 2] = woven, (e - e0) * C

        def copy_on(engine, dst, src):
            if engine == "vector":
                nc.vector.tensor_copy(out=dst, in_=src)
            else:
                nc.scalar.copy(out=dst, in_=src)

        def weave(pair, engine):
            woven, slot0 = woven_of[pair]
            dst = woven[:, 4 * slot0 : 4 * (slot0 + 2 * C)].bitcast(F32).rearrange("p (s v) -> p s v", v=2)
            copy_on(engine, dst, turned_of[pair].rearrange("p v s -> p s v"))

        def quantise(group):
            e0, e1 = QUANTISE[group]
            w = (e1 - e0) * C
            h_words = keep.tile([P, w], U32, name=f"h_words{e0}", align_bytes=64)
            h_scales = keep.tile([P, w], U8, name=f"h_scales{e0}", align_bytes=64)
            nc.vector.quantize_mx(out=h_words[:].bitcast(FP8X4), scales=h_scales[:], in_=woven_of[e0 // 2][0][:])
            for e in range(e0, e1):
                slots = slice((e - e0) * C, (e - e0 + 1) * C)
                codes_of[e] = h_words[:, slots], h_scales[:, slots]

        def second_layer(group, bank, engine):
            e0, e1 = QUANTISE[group]
            for e in range(e0, e1):
                words, scales = codes_of[e]
                nc.tensor.matmul_mx(
                    out=banks[bank][:, (e - e0) * C : (e - e0 + 1) * C],
                    lhsT=w2_of[e].bitcast(FP4X4),
                    lhsT_scale=w2_scales_of[e],
                    rhs=words.bitcast(FP8X4),
                    rhs_scale=scales,
                    start=True,
                    stop=True,
                )
            copy_on(engine, y_sb[:, e0 * C : e1 * C], banks[bank][:, : (e1 - e0) * C])

        for e0, e1 in GATHERS:
            gather(e0, e1)

        for e in range(FIRST_SORTED, E):
            sort_words(e)
        sort_scales()

        for e in range(HALF):
            first_layer(e, e)
        for pair in range(3):
            turn(pair, 4 + pair)
        weave(0, "scalar")
        weave(1, "scalar")
        for e in range(8, 12):
            first_layer(e, e - 8)
        weave(2, "vector")
        quantise(0)
        turn(3, 0)
        turn(4, 1)
        weave(3, "scalar")
        weave(4, "scalar")
        turn(5, 3)
        weave(5, "vector")
        sorted_first_layer(12, 7)
        sorted_first_layer(13, 4)
        sorted_first_layer(14, 5)
        sorted_first_layer(15, 6)
        quantise(1)
        second_layer(0, 7, "vector")
        quantise(2)
        quantise(3)
        quantise(4)
        second_layer(1, 2, "scalar")
        second_layer(2, 0, "scalar")
        second_layer(3, 1, "scalar")
        second_layer(4, 3, "vector")

        def slots_of(choice, t0, w):
            return y_sb[:].indirect(pos_sb[choice][:, t0 // 16 : (t0 + w) // 16])

        widths = SHARED_PIECES + SCALAR_PIECES
        starts = [sum(widths[:k]) for k in range(len(widths))]
        scalar_from = [1] * len(SHARED_PIECES) + [0] * len(SCALAR_PIECES)
        fetched, gated = [], []
        for t0, w, c0 in zip(starts, widths, scalar_from):
            fetched.append(keep.tile([P, 2 - c0, w], F32, name=f"fetched{t0}"))
            gated.append(keep.tile([P, 2 - c0, w], F32, name=f"gated{t0}"))
            for choice in range(c0, 2):
                nc.scalar.activation(fetched[-1][:, choice - c0, :], slots_of(choice, t0, w), COPY)

        shared = sum(SHARED_PIECES)
        first_gated = keep.tile([P, shared], F32, name="first_gated")

        def apply_gate(k):
            t0, w, c0 = starts[k], widths[k], scalar_from[k]
            nc.vector.tensor_tensor(gated[k][:], fetched[k][:], gate_sb[:, c0:, t0 : t0 + w], MULT)

        def add_and_store(k):
            t0, w, c0 = starts[k], widths[k], scalar_from[k]
            result = keep.tile([P, w], F32, name=f"result{t0}")
            first = first_gated[:, t0 : t0 + w] if c0 == 1 else gated[k][:, 0, :]
            nc.vector.tensor_tensor(result[:], first, gated[k][:, 1 - c0, :], ADD)
            queue = nc.scalar if k >= len(SHARED_PIECES) else nc.sync
            queue.dma_start(out=out[:, t0 : t0 + w], in_=result[:])

        nc.vector.tensor_tensor(first_gated[:], slots_of(0, 0, shared), gate_sb[:, 0, :shared], MULT)
        for k in range(len(SHARED_PIECES)):
            apply_gate(k)
        for k in range(len(SHARED_PIECES)):
            add_and_store(k)
        apply_gate(len(SHARED_PIECES))
        for k in range(len(SHARED_PIECES) + 1, len(widths)):
            apply_gate(k)
            add_and_store(k - 1)
        add_and_store(len(widths) - 1)
